import numpy as np
import ml_dtypes


def mxq(x, axis, fmt="e4m3"):
    dtype, down = {"e4m3": (ml_dtypes.float8_e4m3fn, 7), "e5m2": (ml_dtypes.float8_e5m2, 14)}[fmt]
    v = np.moveaxis(np.asarray(x, np.float32).astype(ml_dtypes.bfloat16).astype(np.float64), axis, -1)
    blocks = v.reshape(v.shape[:-1] + (-1, 32))
    amax = np.abs(blocks).max(-1, keepdims=True)
    byte = np.maximum(np.where(amax > 0, np.frexp(amax)[1] - 1 + 127, 0) - down, 1)
    scale = np.exp2(byte - 127.0)
    codes = (blocks / scale).astype(np.float32).astype(dtype).astype(np.float64)
    return np.moveaxis((codes * scale).reshape(v.shape), -1, axis)


WIDE = False


def mx_kscale(k):
    if not WIDE:
        return np.ones(k)
    levels = np.array([10, -10, 5, -5, 0])
    if k % 512:
        return np.exp2(np.random.permutation(np.resize(levels, k // 32))).repeat(32)
    a = np.empty((k // 512, 16))
    for p in range(k // 512):
        a[p, :8] = np.random.permutation(np.resize(levels, 8))
        for g in range(8):
            far = levels[np.abs(levels - a[p, g]) >= 10]
            a[p, g + 8] = far[np.random.randint(len(far))]
    return np.exp2(a.ravel()).repeat(32)


BF16 = ml_dtypes.bfloat16


def bf(x):
    return np.asarray(x, np.float32).astype(BF16)


def f64(x):
    return np.asarray(x).astype(np.float64)


E2M1 = np.array([0.0, 0.5, 1.0, 1.5, 2.0, 3.0, 4.0, 6.0, -0.0, -0.5, -1.0, -1.5, -2.0, -3.0, -4.0, -6.0])


def pack_weight(w, fmt):
    k, n = w.shape
    w = f64(bf(w)).reshape(k // 32, 32, n)
    amax = np.abs(w).max(1)
    if fmt == "e4m3":
        byte = np.frexp(amax)[1] - 1 + 127 - 7
    else:
        mant, ex = np.frexp(amax / 6.0)
        byte = np.where(mant > 0.5, ex, ex - 1) + 127
    byte = np.clip(np.where(amax > 0, byte, 1), 1, 254)
    scaled = (w * np.exp2(127.0 - byte)[:, None, :]).reshape(k, n).astype(np.float32)
    by_word = np.ascontiguousarray(scaled.reshape(k // 512, 128, 4, n).transpose(0, 1, 3, 2))
    if fmt == "e4m3":
        words = by_word.astype(ml_dtypes.float8_e4m3fn).view(np.uint8)
    else:
        c = by_word.astype(ml_dtypes.float4_e2m1fn).view(np.uint8) & 0xF
        words = c[..., 0::2] | (c[..., 1::2] << 4)
    return np.ascontiguousarray(words), np.ascontiguousarray(byte.astype(np.uint8).reshape(k // 512, 16, n))


def unpack_weight(words, scales, fmt):
    g, p, n, _ = words.shape
    if fmt == "e4m3":
        vals = np.ascontiguousarray(words).view(ml_dtypes.float8_e4m3fn).astype(np.float64)
    else:
        nib = np.empty((g, p, n, 4), np.uint8)
        nib[..., 0::2] = words & 0xF
        nib[..., 1::2] = words >> 4
        vals = E2M1[nib]
    vals = vals * np.repeat(np.exp2(scales.astype(np.float64) - 127.0), 8, axis=1)[..., None]
    return vals.transpose(0, 1, 3, 2).reshape(g * 512, n)
def pack4(w):
    words, scales = pack_weight(w, "e2m1")
    return words.reshape(words.shape[0], 128, -1), scales


def unpack4(words, scales):
    return unpack_weight(words.reshape(words.shape[0], 128, -1, 2), scales, "e2m1")


def planes(Y):
    n, m = Y.shape
    b = f64(bf(Y)).reshape(n // 32, 32, m)
    amax = np.abs(b).max(1)
    byte = np.clip(np.where(amax > 0, np.frexp(amax)[1] - 1 + 127 - 7, 1), 1, 254)
    codes = (b * np.exp2(127.0 - byte)[:, None, :]).reshape(n, m).astype(np.float32).astype(ml_dtypes.float8_e4m3fn).view(np.uint8)
    words = codes.reshape(n // 512, 128, 4, m).transpose(0, 1, 3, 2)
    return np.ascontiguousarray(words), np.ascontiguousarray(byte.astype(np.uint8).reshape(n // 512, 16, m))


B, R, U = 1024, 1536, 512
RECUR = 0.9
DRIVE = 0.7

def setup_inputs():
    s = mx_kscale(R)
    v = mx_kscale(U)
    amp = np.exp(0.8 * np.random.randn(R))
    h = np.tanh(np.random.randn(B, R)) * amp
    u = np.random.randn(B, U)
    wr = RECUR * np.random.randn(R, R) / np.sqrt(R)
    win = DRIVE * np.random.randn(U, R) / np.sqrt(U)
    wr_words, wr_scales = pack4(wr / s[:, None])
    win_words, win_scales = pack4(win / v[:, None])
    return {
        "h": bf(h * s),
        "u": bf(u * v),
        "wr_words": wr_words,
        "wr_scales": wr_scales,
        "win_words": win_words,
        "win_scales": win_scales,
        "bias": bf(0.3 * np.random.randn(R)),
        "amp": bf(amp),
    }

def reference(h, u, wr_words, wr_scales, win_words, win_scales, bias, amp):
    wr = unpack4(wr_words, wr_scales)
    win = unpack4(win_words, win_scales)
    recurrent = mxq(f64(h), 1, "e4m3") @ wr
    driven = mxq(f64(u), 1, "e4m3") @ win
    y = np.tanh(recurrent + driven + f64(bias)) * f64(amp)
    Y = y.T
    words, scales = planes(Y)
    return y, words, scales

@@ -1,0 +1,313 @@
+from contextlib import ExitStack
+
+import concourse.mybir as mybir
+from concourse.masks import make_identity
+
+B, R, U = 1024, 1536, 512
+FLOPS = 2 * B * (R + U) * R
+
+F32 = mybir.dt.float32
+BF16 = mybir.dt.bfloat16
+I32 = mybir.dt.int32
+U32 = mybir.dt.uint32
+U8 = mybir.dt.uint8
+FP8X4 = mybir.dt.float8_e4m3fn_x4
+FP4X4 = mybir.dt.float4_e2m1fn_x4
+ALU = mybir.AluOpType
+ACT = mybir.ActivationFunctionType
+
+P = 128
+K_PASS = 512
+TILES = B // P
+CHUNKS = R // K_PASS
+LAST = TILES - 1
+
+
+def tile_reservoir_state_step_g4_kernel(
+    tc, h, u, wr_words, wr_scales, win_words, win_scales, bias, amp, out_0, out_1, out_2
+):
+    nc = tc.nc
+    with ExitStack() as ctx:
+        keep = ctx.enter_context(tc.tile_pool(name="keep", bufs=1))
+        work = ctx.enter_context(tc.tile_pool(name="work", bufs=4))
+        psum = ctx.enter_context(tc.psum_pool(name="psum", bufs=1))
+        ctx.enter_context(tc.manual_schedule())
+
+        ident = keep.tile([P, P], F32, name="ident")
+        make_identity(nc, ident[:])
+
+        wr_sc = keep.tile([P, CHUNKS, R], U8, name="wr_sc", align_bytes=64)
+        win_sc = keep.tile([P, R], U8, name="win_sc", align_bytes=64)
+        nc.vector.memset(wr_sc[:].bitcast(I32), 0)
+        nc.vector.memset(win_sc[:].bitcast(I32), 0)
+
+        def load_column(label, vec):
+            col = keep.tile([P, CHUNKS, 4], BF16, name=label)
+            nc.sync.dma_start(out=col[:], in_=vec.rearrange("(c p e) -> p c e", c=CHUNKS, e=4))
+            return col
+
+        x_raw = {}
+
+        def load_x(t, spans):
+            rows = slice(t * P, (t + 1) * P)
+            for src, g0, first, count in spans:
+                raw = keep.tile([P, count * K_PASS], BF16, name="x_raw_%d_%d" % (t, g0))
+                nc.sync.dma_start(out=raw[:], in_=src[rows, first * K_PASS : (first + count) * K_PASS])
+                for i in range(count):
+                    x_raw[t, g0 + i] = raw[:].bitcast(F32)[:, i * 256 : (i + 1) * 256]
+
+        w_codes = {}
+
+        def load_wr(c):
+            w = keep.tile([P, CHUNKS, 1024], U8, name="wr_%d" % c, align_bytes=64)
+            src = wr_words[:, :, c * 1024 : (c + 1) * 1024].rearrange("g p n -> p g n")
+            nc.sync.dma_start(out=w[:].bitcast(I32), in_=src.bitcast(I32))
+            for g in range(CHUNKS):
+                w_codes[g, c] = w[:, g, :]
+
+        def load_win(c):
+            w = keep.tile([P, 1024], U8, name="win_%d" % c, align_bytes=64)
+            nc.sync.dma_start(out=w[:].bitcast(I32), in_=win_words[0, :, c * 1024 : (c + 1) * 1024].bitcast(I32))
+            w_codes[CHUNKS, c] = w[:]
+
+        bias_col = load_column("bias_col", bias)
+        load_x(0, [(h, 0, 0, 2), (h, 2, 2, 1), (u, 3, 0, 1)])
+        for q in range(4):
+            src = wr_scales[:, 4 * q : 4 * q + 4, :].rearrange("g r n -> r g n")
+            nc.sync.dma_start(out=wr_sc[32 * q : 32 * q + 4].bitcast(I32), in_=src.bitcast(I32))
+        load_wr(0)
+        for q in range(4):
+            src = win_scales[0, 4 * q : 4 * q + 4, :]
+            nc.gpsimd.dma_start(out=win_sc[32 * q : 32 * q + 4].bitcast(I32), in_=src.bitcast(I32))
+        load_win(0)
+        amp_col = load_column("amp_col", amp)
+        whole = [(h, 0, 0, CHUNKS), (u, CHUNKS, 0, 1)]
+        load_x(1, whole)
+        for c in range(1, CHUNKS):
+            load_wr(c)
+            load_win(c)
+        for t in range(2, TILES):
+            load_x(t, whole)
+
+        def w_scale(g, c):
+            cols = slice(c * K_PASS, (c + 1) * K_PASS)
+            return wr_sc[:, g, cols] if g < CHUNKS else win_sc[:, cols]
+
+        def copy(engine, out, in_):
+            if engine is nc.scalar:
+                nc.scalar.copy(out=out, in_=in_)
+            else:
+                nc.vector.tensor_copy(out=out, in_=in_)
+
+        def interleave(engine, dst, bank, groups):
+            copy(
+                engine,
+                dst.bitcast(F32).rearrange("p (g r u) -> p g r u", g=groups, u=2),
+                bank[:, : groups * 256].rearrange("p (g u r) -> p g r u", g=groups, u=2),
+            )
+
+        x_bank, x_grouped, x_codes, x_scales = {}, {}, {}, {}
+
+        def x_transposes(t):
+            for half in range(2):
+                bank = psum.tile([P, 512], F32, name="x_bank_%d" % half)
+                for i in range(2):
+                    words = x_raw[t, 2 * half + i]
+                    for w in range(2):
+                        at = (2 * i + w) * P
+                        nc.tensor.transpose(bank[:, at : at + P], words[:, w::2], ident[:])
+                x_bank[t, half] = bank
+
+        def x_copy(t, half, engine):
+            grouped = work.tile([P, 1024], BF16, name="x_grouped", align_bytes=64)
+            interleave(engine, grouped[:], x_bank[t, half], 2)
+            x_grouped[t, half] = grouped
+
+        def x_quantize(t, half):
+            codes = work.tile([P, 256], U32, name="x_codes", align_bytes=64, bufs=8)
+            scales = work.tile([P, 256], U8, name="x_scales", align_bytes=64, bufs=8)
+            nc.vector.quantize_mx(out=codes[:].bitcast(FP8X4), scales=scales[:], in_=x_grouped[t, half][:])
+            for i in range(2):
+                x_codes[t, 2 * half + i] = codes[:, i * P : (i + 1) * P]
+                x_scales[t, 2 * half + i] = scales[:, i * P : (i + 1) * P]
+
+        def spread(col, rows):
+            words = col[:].bitcast(F32)
+            for part, chunks in enumerate(((0, 1), (2,))):
+                bank = psum.tile([P, 512], F32, name="y_bank_%d" % part)
+                for i, c in enumerate(chunks):
+                    for w in range(2):
+                        at = (2 * i + w) * P
+                        nc.tensor.transpose(bank[:, at : at + P], words[:, c, w : w + 1].to_broadcast([P, P]), ident[:])
+                interleave(nc.scalar, rows[:, part * 1024 : part * 1024 + len(chunks) * K_PASS], bank, len(chunks))
+
+        acc, pre, y_rows, y_bf, y_bank, y_grouped, y_codes = {}, {}, {}, {}, {}, {}, {}
+
+        def matmuls(t, c):
+            bank = psum.tile([P, 512], F32, name="acc", bufs=4)
+            for g in range(CHUNKS + 1):
+                nc.tensor.matmul_mx(
+                    out=bank[:],
+                    lhsT=x_codes[t, g].bitcast(FP8X4),
+                    lhsT_scale=x_scales[t, g],
+                    rhs=w_codes[g, c].bitcast(FP4X4),
+                    rhs_scale=w_scale(g, c),
+                    start=(g == 0),
+                    stop=(g == CHUNKS),
+                )
+            acc[t, c] = bank
+
+        def add_bias(t, c, lo=0, hi=K_PASS):
+            if lo == 0:
+                pre[t, c] = work.tile([P, K_PASS], F32, name="pre")
+            nc.vector.tensor_tensor(
+                out=pre[t, c][:, lo:hi],
+                in0=acc[t, c][:, lo:hi],
+                in1=bias_rows[:, c * K_PASS + lo : c * K_PASS + hi],
+                op=ALU.add,
+            )
+
+        def tanh(t, c, lo=0, hi=K_PASS):
+            nc.scalar.activation(out=pre[t, c][:, lo:hi], in_=pre[t, c][:, lo:hi], func=ACT.Tanh)
+
+        def scale(t, c, lo=0, hi=K_PASS):
+            if (t, c, lo) == (t, 0, 0):
+                y_rows[t] = work.tile([P, R], F32, name="y_rows")
+            cols = slice(c * K_PASS + lo, c * K_PASS + hi)
+            nc.vector.tensor_tensor(out=y_rows[t][:, cols], in0=pre[t, c][:, lo:hi], in1=amp_rows[:, cols], op=ALU.mult)
+
+        def store_y(t, first, last):
+            cols = slice(first * K_PASS, last * K_PASS)
+            nc.sync.dma_start(out=out_0[t * P : (t + 1) * P, cols], in_=y_rows[t][:, cols])
+
+        def round_y(t, c, engine, lo=0, hi=K_PASS):
+            if lo == 0:
+                y_bf[t, c] = work.tile([P, K_PASS], BF16, name="y_bf", bufs=6)
+            dst = y_bf[t, c][:].rearrange("p (w a b e) -> p a w b e", w=2, b=4, e=2)
+            src = y_rows[t][:, c * K_PASS : (c + 1) * K_PASS].rearrange("p (a b w e) -> p a w b e", b=4, w=2, e=2)
+            copy(engine, dst[:, lo // 16 : hi // 16], src[:, lo // 16 : hi // 16])
+
+        def y_transposes(t, part):
+            bank = psum.tile([P, 512], F32, name="y_bank_%d" % part)
+            for i, c in enumerate((0, 1) if part == 0 else (2,)):
+                words = y_bf[t, c][:].bitcast(F32)
+                for w in range(2):
+                    at = (2 * i + w) * P
+                    nc.tensor.transpose(bank[:, at : at + P], words[:, w * P : (w + 1) * P], ident[:])
+            y_bank[t, part] = bank
+
+        def y_copy(t, part, engine):
+            groups = 2 - part
+            grouped = work.tile([P, groups * K_PASS], BF16, name="y_grouped_%d" % part, align_bytes=64, bufs=2)
+            interleave(engine, grouped[:], y_bank[t, part], groups)
+            for i in range(groups):
+                y_grouped[t, 2 * part + i] = grouped[:, i * K_PASS : (i + 1) * K_PASS]
+
+        early_scales = keep.tile([P, CHUNKS, LAST * P], U8, name="early_scales", align_bytes=64)
+        last_scales = keep.tile([P, CHUNKS, P], U8, name="last_scales", align_bytes=64)
+
+        def y_quantize(t, c):
+            if c == 0:
+                y_codes[t] = work.tile([P, CHUNKS, P], U32, name="y_codes", align_bytes=64)
+            scales = last_scales[:, c, :] if t == LAST else early_scales[:, c, t * P : (t + 1) * P]
+            nc.vector.quantize_mx(out=y_codes[t][:, c, :].bitcast(FP8X4), scales=scales, in_=y_grouped[t, c])
+
+        def store_codes(t, first, last):
+            dst = out_1.rearrange("g p m t -> p g (m t)")[:, first:last, t * 4 * P : (t + 1) * 4 * P]
+            nc.sync.dma_start(out=dst.bitcast(I32), in_=y_codes[t][:, first:last, :].bitcast(I32))
+
+        def store_scales(scales, lo, hi, engines):
+            for q in range(4):
+                dst = out_2[:, 4 * q : 4 * q + 4, lo:hi].rearrange("g r m -> r g m")
+                engines[q].dma_start(out=dst.bitcast(I32), in_=scales[32 * q : 32 * q + 4].bitcast(I32))
+
+        bias_rows = keep.tile([P, R], BF16, name="bias_rows")
+        amp_rows = keep.tile([P, R], BF16, name="amp_rows")
+        spread(bias_col, bias_rows)
+        x_transposes(0)
+        x_copy(0, 0, nc.scalar)
+        x_quantize(0, 0)
+        x_copy(0, 1, nc.scalar)
+        x_quantize(0, 1)
+
+        for t in range(TILES):
+            matmuls(t, 0)
+            if t >= 1:
+                add_bias(t - 1, 2)
+            if t >= 2:
+                y_copy(t - 2, 1, nc.scalar)
+            if t >= 1:
+                tanh(t - 1, 2)
+                scale(t - 1, 1)
+                round_y(t - 1, 0, nc.scalar)
+            add_bias(t, 0)
+            if t == 0:
+                x_transposes(1)
+                spread(amp_col, amp_rows)
+            matmuls(t, 1)
+            if t >= 1:
+                scale(t - 1, 2)
+                store_y(t - 1, 0, CHUNKS)
+            tanh(t, 0)
+            if t >= 1:
+                round_y(t - 1, 2, nc.scalar)
+            else:
+                x_copy(1, 0, nc.scalar)
+                x_copy(1, 1, nc.scalar)
+            add_bias(t, 1)
+            if t >= 1:
+                round_y(t - 1, 1, nc.vector)
+            tanh(t, 1)
+            scale(t, 0)
+            if t == 0:
+                x_quantize(1, 0)
+                x_quantize(1, 1)
+            if t >= 2:
+                for c in range(CHUNKS):
+                    y_quantize(t - 2, c)
+                store_codes(t - 2, 0, CHUNKS)
+            if t + 2 < TILES:
+                x_transposes(t + 2)
+            if t >= 1:
+                y_transposes(t - 1, 0)
+                y_transposes(t - 1, 1)
+            matmuls(t, 2)
+            if t + 2 < TILES:
+                x_copy(t + 2, 0, nc.scalar)
+                x_copy(t + 2, 1, nc.scalar)
+            if t >= 1:
+                y_copy(t - 1, 0, nc.scalar)
+            if t + 2 < TILES:
+                x_quantize(t + 2, 0)
+                x_quantize(t + 2, 1)
+
+        t = LAST
+        y_copy(t - 1, 1, nc.scalar)
+        store_y(t, 0, 1)
+        scale(t, 1)
+        store_y(t, 1, 2)
+        round_y(t, 0, nc.scalar)
+        y_quantize(t - 1, 0)
+        y_quantize(t - 1, 1)
+        round_y(t, 1, nc.scalar)
+        y_transposes(t, 0)
+        halves = ((0, 256), (256, 512))
+        for lo, hi in halves:
+            add_bias(t, 2, lo, hi)
+            tanh(t, 2, lo, hi)
+        y_quantize(t - 1, 2)
+        store_codes(t - 1, 0, CHUNKS)
+        store_scales(early_scales, 0, LAST * P, [nc.sync] * 4)
+        for lo, hi in halves:
+            scale(t, 2, lo, hi)
+            round_y(t, 2, nc.scalar, lo, hi)
+        store_y(t, 2, 3)
+        y_copy(t, 0, nc.vector)
+        y_transposes(t, 1)
+        y_copy(t, 1, nc.scalar)
+        y_quantize(t, 0)
+        y_quantize(t, 1)
+        store_codes(t, 0, 2)
+        y_quantize(t, 2)
+        store_codes(t, 2, 3)
+        store_scales(last_scales, LAST * P, B, [nc.sync, nc.scalar, nc.sync, nc.scalar])

@@ -21,6 +21,8 @@ K_PASS = 512
 TILES = B // P
 CHUNKS = R // K_PASS
 LAST = TILES - 1
+LOW, HIGH = (0, 1), (2, 3)
+EARLY = TILES - 2
 
 
 def tile_reservoir_state_step_g4_kernel(
@@ -65,27 +67,27 @@ def tile_reservoir_state_step_g4_kernel(
             for g in range(CHUNKS):
                 w_codes[g, c] = w[:, g, :]
 
-        def load_win(c):
-            w = keep.tile([P, 1024], U8, name="win_%d" % c, align_bytes=64)
-            nc.sync.dma_start(out=w[:].bitcast(I32), in_=win_words[0, :, c * 1024 : (c + 1) * 1024].bitcast(I32))
-            w_codes[CHUNKS, c] = w[:]
+        def load_win():
+            w = keep.tile([P, 2 * R], U8, name="win", align_bytes=64)
+            nc.sync.dma_start(out=w[:].bitcast(I32), in_=win_words[0].bitcast(I32))
+            for c in range(CHUNKS):
+                w_codes[CHUNKS, c] = w[:, c * 1024 : (c + 1) * 1024]
 
+        whole = [(h, 0, 0, CHUNKS), (u, CHUNKS, 0, 1)]
         bias_col = load_column("bias_col", bias)
-        load_x(0, [(h, 0, 0, 2), (h, 2, 2, 1), (u, 3, 0, 1)])
+        load_x(0, whole)
         for q in range(4):
             src = wr_scales[:, 4 * q : 4 * q + 4, :].rearrange("g r n -> r g n")
-            nc.sync.dma_start(out=wr_sc[32 * q : 32 * q + 4].bitcast(I32), in_=src.bitcast(I32))
+            nc.scalar.dma_start(out=wr_sc[32 * q : 32 * q + 4].bitcast(I32), in_=src.bitcast(I32))
         load_wr(0)
+        load_win()
+        load_x(1, whole)
         for q in range(4):
             src = win_scales[0, 4 * q : 4 * q + 4, :]
-            nc.gpsimd.dma_start(out=win_sc[32 * q : 32 * q + 4].bitcast(I32), in_=src.bitcast(I32))
-        load_win(0)
+            nc.sync.dma_start(out=win_sc[32 * q : 32 * q + 4].bitcast(I32), in_=src.bitcast(I32))
+        load_wr(1)
+        load_wr(2)
         amp_col = load_column("amp_col", amp)
-        whole = [(h, 0, 0, CHUNKS), (u, CHUNKS, 0, 1)]
-        load_x(1, whole)
-        for c in range(1, CHUNKS):
-            load_wr(c)
-            load_win(c)
         for t in range(2, TILES):
             load_x(t, whole)
 
@@ -108,28 +110,30 @@ def tile_reservoir_state_step_g4_kernel(
 
         x_bank, x_grouped, x_codes, x_scales = {}, {}, {}, {}
 
-        def x_transposes(t):
-            for half in range(2):
-                bank = psum.tile([P, 512], F32, name="x_bank_%d" % half)
-                for i in range(2):
-                    words = x_raw[t, 2 * half + i]
-                    for w in range(2):
-                        at = (2 * i + w) * P
-                        nc.tensor.transpose(bank[:, at : at + P], words[:, w::2], ident[:])
-                x_bank[t, half] = bank
+        def x_transposes(t, passes, name):
+            bank = psum.tile([P, 512], F32, name=name, bufs=4 if name == "acc" else 1)
+            for i, g in enumerate(passes):
+                for w in range(2):
+                    at = (2 * i + w) * P
+                    nc.tensor.transpose(bank[:, at : at + P], x_raw[t, g][:, w::2], ident[:])
+            x_bank[t, passes] = bank
 
-        def x_copy(t, half, engine):
-            grouped = work.tile([P, 1024], BF16, name="x_grouped", align_bytes=64)
-            interleave(engine, grouped[:], x_bank[t, half], 2)
-            x_grouped[t, half] = grouped
+        def x_copy(t, passes, engine):
+            grouped = work.tile([P, len(passes) * K_PASS], BF16, name="x_grouped", align_bytes=64)
+            interleave(engine, grouped[:], x_bank[t, passes], len(passes))
+            x_grouped[t, passes] = grouped
 
-        def x_quantize(t, half):
-            codes = work.tile([P, 256], U32, name="x_codes", align_bytes=64, bufs=8)
-            scales = work.tile([P, 256], U8, name="x_scales", align_bytes=64, bufs=8)
-            nc.vector.quantize_mx(out=codes[:].bitcast(FP8X4), scales=scales[:], in_=x_grouped[t, half][:])
-            for i in range(2):
-                x_codes[t, 2 * half + i] = codes[:, i * P : (i + 1) * P]
-                x_scales[t, 2 * half + i] = scales[:, i * P : (i + 1) * P]
+        def x_quantize(t, passes):
+            codes = work.tile([P, len(passes) * P], U32, name="x_codes", align_bytes=64, bufs=8)
+            scales = work.tile([P, len(passes) * P], U8, name="x_scales", align_bytes=64, bufs=8)
+            nc.vector.quantize_mx(out=codes[:].bitcast(FP8X4), scales=scales[:], in_=x_grouped[t, passes][:])
+            for i, g in enumerate(passes):
+                x_codes[t, g] = codes[:, i * P : (i + 1) * P]
+                x_scales[t, g] = scales[:, i * P : (i + 1) * P]
+
+        def x_run(t):
+            x_transposes(t, LOW, "x_bank_0")
+            x_transposes(t, HIGH, "x_bank_1")
 
         def spread(col, rows):
             words = col[:].bitcast(F32)
@@ -170,11 +174,11 @@ def tile_reservoir_state_step_g4_kernel(
         def tanh(t, c, lo=0, hi=K_PASS):
             nc.scalar.activation(out=pre[t, c][:, lo:hi], in_=pre[t, c][:, lo:hi], func=ACT.Tanh)
 
-        def scale(t, c, lo=0, hi=K_PASS):
+        def scale(t, c, engine, lo=0, hi=K_PASS):
             if (t, c, lo) == (t, 0, 0):
                 y_rows[t] = work.tile([P, R], F32, name="y_rows")
             cols = slice(c * K_PASS + lo, c * K_PASS + hi)
-            nc.vector.tensor_tensor(out=y_rows[t][:, cols], in0=pre[t, c][:, lo:hi], in1=amp_rows[:, cols], op=ALU.mult)
+            engine.tensor_tensor(out=y_rows[t][:, cols], in0=pre[t, c][:, lo:hi], in1=amp_rows[:, cols], op=ALU.mult)
 
         def store_y(t, first, last):
             cols = slice(first * K_PASS, last * K_PASS)
@@ -187,29 +191,40 @@ def tile_reservoir_state_step_g4_kernel(
             src = y_rows[t][:, c * K_PASS : (c + 1) * K_PASS].rearrange("p (a b w e) -> p a w b e", b=4, w=2, e=2)
             copy(engine, dst[:, lo // 16 : hi // 16], src[:, lo // 16 : hi // 16])
 
-        def y_transposes(t, part):
-            bank = psum.tile([P, 512], F32, name="y_bank_%d" % part)
-            for i, c in enumerate((0, 1) if part == 0 else (2,)):
+        def scale_round(t, c, lo, hi):
+            if lo == 0:
+                y_bf[t, c] = work.tile([P, K_PASS], BF16, name="y_bf", bufs=6)
+            words = slice(lo // 4, hi // 4)
+            nc.vector.tensor_tensor(
+                out=y_bf[t, c][:].rearrange("p (w j e) -> p w j e", w=2, e=2)[:, :, words],
+                in0=pre[t, c][:].rearrange("p (j w e) -> p w j e", w=2, e=2)[:, :, words],
+                in1=amp_rows[:, c * K_PASS : (c + 1) * K_PASS].rearrange("p (j w e) -> p w j e", w=2, e=2)[:, :, words],
+                op=ALU.mult,
+            )
+
+        def y_transposes(t, chunks, name):
+            bank = psum.tile([P, 512], F32, name=name)
+            for i, c in enumerate(chunks):
                 words = y_bf[t, c][:].bitcast(F32)
                 for w in range(2):
                     at = (2 * i + w) * P
                     nc.tensor.transpose(bank[:, at : at + P], words[:, w * P : (w + 1) * P], ident[:])
-            y_bank[t, part] = bank
+            y_bank[t, chunks] = bank
 
-        def y_copy(t, part, engine):
-            groups = 2 - part
-            grouped = work.tile([P, groups * K_PASS], BF16, name="y_grouped_%d" % part, align_bytes=64, bufs=2)
-            interleave(engine, grouped[:], y_bank[t, part], groups)
-            for i in range(groups):
-                y_grouped[t, 2 * part + i] = grouped[:, i * K_PASS : (i + 1) * K_PASS]
+        def y_copy(t, chunks, engine):
+            grouped = work.tile([P, len(chunks) * K_PASS], BF16, name="y_grouped", align_bytes=64, bufs=6)
+            interleave(engine, grouped[:], y_bank[t, chunks], len(chunks))
+            for i, c in enumerate(chunks):
+                y_grouped[t, c] = grouped[:, i * K_PASS : (i + 1) * K_PASS]
 
-        early_scales = keep.tile([P, CHUNKS, LAST * P], U8, name="early_scales", align_bytes=64)
-        last_scales = keep.tile([P, CHUNKS, P], U8, name="last_scales", align_bytes=64)
+        early_scales = keep.tile([P, CHUNKS, EARLY * P], U8, name="early_scales", align_bytes=64)
+        last_scales = keep.tile([P, CHUNKS, B - EARLY * P], U8, name="last_scales", align_bytes=64)
 
         def y_quantize(t, c):
-            if c == 0:
+            if t not in y_codes:
                 y_codes[t] = work.tile([P, CHUNKS, P], U32, name="y_codes", align_bytes=64)
-            scales = last_scales[:, c, :] if t == LAST else early_scales[:, c, t * P : (t + 1) * P]
+            plane, at = (early_scales, t * P) if t < EARLY else (last_scales, (t - EARLY) * P)
+            scales = plane[:, c, at : at + P]
             nc.vector.quantize_mx(out=y_codes[t][:, c, :].bitcast(FP8X4), scales=scales, in_=y_grouped[t, c])
 
         def store_codes(t, first, last):
@@ -224,90 +239,101 @@ def tile_reservoir_state_step_g4_kernel(
         bias_rows = keep.tile([P, R], BF16, name="bias_rows")
         amp_rows = keep.tile([P, R], BF16, name="amp_rows")
         spread(bias_col, bias_rows)
-        x_transposes(0)
-        x_copy(0, 0, nc.scalar)
-        x_quantize(0, 0)
-        x_copy(0, 1, nc.scalar)
-        x_quantize(0, 1)
+        for g, name in enumerate(("x_bank_0", "x_bank_1", "acc", "acc")):
+            x_transposes(0, (g,), name)
+        for g in range(CHUNKS + 1):
+            x_copy(0, (g,), nc.vector if g % 2 == 0 else nc.scalar)
+            if g % 2 == 1:
+                x_quantize(0, (g - 1,))
+                x_quantize(0, (g,))
 
         for t in range(TILES):
+            more_x = t + 2 < TILES
             matmuls(t, 0)
             if t >= 1:
-                add_bias(t - 1, 2)
-            if t >= 2:
-                y_copy(t - 2, 1, nc.scalar)
-            if t >= 1:
-                tanh(t - 1, 2)
-                scale(t - 1, 1)
                 round_y(t - 1, 0, nc.scalar)
+                add_bias(t - 1, 2)
+                tanh(t - 1, 2)
+                scale(t - 1, 1, nc.vector)
+                round_y(t - 1, 1, nc.scalar)
             add_bias(t, 0)
             if t == 0:
-                x_transposes(1)
+                x_run(1)
                 spread(amp_col, amp_rows)
             matmuls(t, 1)
             if t >= 1:
-                scale(t - 1, 2)
+                scale(t - 1, 2, nc.vector)
                 store_y(t - 1, 0, CHUNKS)
             tanh(t, 0)
-            if t >= 1:
-                round_y(t - 1, 2, nc.scalar)
-            else:
-                x_copy(1, 0, nc.scalar)
-                x_copy(1, 1, nc.scalar)
-            add_bias(t, 1)
-            if t >= 1:
-                round_y(t - 1, 1, nc.vector)
-            tanh(t, 1)
-            scale(t, 0)
             if t == 0:
-                x_quantize(1, 0)
-                x_quantize(1, 1)
+                x_copy(1, LOW, nc.vector)
+                x_copy(1, HIGH, nc.vector)
+            add_bias(t, 1)
+            scale(t, 0, nc.vector)
+            if t == 0:
+                x_quantize(1, LOW)
+                x_quantize(1, HIGH)
+            if t >= 1:
+                round_y(t - 1, 2, nc.vector if more_x else nc.scalar)
+            if more_x:
+                x_run(t + 2)
+            if t >= 1:
+                y_transposes(t - 1, LOW, "y_bank_0")
             if t >= 2:
-                for c in range(CHUNKS):
-                    y_quantize(t - 2, c)
-                store_codes(t - 2, 0, CHUNKS)
-            if t + 2 < TILES:
-                x_transposes(t + 2)
-            if t >= 1:
-                y_transposes(t - 1, 0)
-                y_transposes(t - 1, 1)
+                y_transposes(t - 2, (2,), "y_bank_1")
             matmuls(t, 2)
-            if t + 2 < TILES:
-                x_copy(t + 2, 0, nc.scalar)
-                x_copy(t + 2, 1, nc.scalar)
-            if t >= 1:
-                y_copy(t - 1, 0, nc.scalar)
-            if t + 2 < TILES:
-                x_quantize(t + 2, 0)
-                x_quantize(t + 2, 1)
+            if more_x:
+                x_copy(t + 2, LOW, nc.scalar)
+            if t == LAST:
+                y_copy(t - 2, (2,), nc.scalar)
+            tanh(t, 1)
+            if more_x:
+                x_quantize(t + 2, LOW)
+                x_copy(t + 2, HIGH, nc.scalar)
+            if t >= 2:
+                y_quantize(t - 2, 0)
+                y_quantize(t - 2, 1)
+            if t >= 3:
+                y_quantize(t - 3, 2)
+                store_codes(t - 3, 0, CHUNKS)
+            if more_x:
+                x_quantize(t + 2, HIGH)
+            if 1 <= t < LAST:
+                y_copy(t - 1, LOW, nc.scalar)
+            if 2 <= t < LAST:
+                y_copy(t - 2, (2,), nc.scalar)
+        y_quantize(LAST - 2, 2)
+        store_codes(LAST - 2, 0, CHUNKS)
+        store_scales(early_scales, 0, EARLY * P, [nc.sync] * 4)
 
         t = LAST
-        y_copy(t - 1, 1, nc.scalar)
-        store_y(t, 0, 1)
-        scale(t, 1)
-        store_y(t, 1, 2)
-        round_y(t, 0, nc.scalar)
-        y_quantize(t - 1, 0)
-        y_quantize(t - 1, 1)
-        round_y(t, 1, nc.scalar)
-        y_transposes(t, 0)
         halves = ((0, 256), (256, 512))
+        round_y(t, 0, nc.scalar)
+        y_transposes(t - 1, (2,), "x_bank_0")
+        y_transposes(t, (0,), "x_bank_1")
         for lo, hi in halves:
             add_bias(t, 2, lo, hi)
             tanh(t, 2, lo, hi)
+        scale(t, 1, nc.vector)
+        store_y(t, 0, 2)
+        round_y(t, 1, nc.scalar)
+        for lo, hi in halves:
+            scale_round(t, 2, lo, hi)
+        y_transposes(t, (2,), "y_bank_1")
+        y_copy(t - 1, LOW, nc.scalar)
+        y_transposes(t, (1,), "y_bank_0")
+        scale(t, 2, nc.vector)
+        store_y(t, 2, 3)
+        y_copy(t - 1, (2,), nc.vector)
+        y_copy(t, (2,), nc.scalar)
+        y_copy(t, (0,), nc.vector)
+        y_quantize(t - 1, 0)
+        y_quantize(t - 1, 1)
+        y_copy(t, (1,), nc.scalar)
         y_quantize(t - 1, 2)
         store_codes(t - 1, 0, CHUNKS)
-        store_scales(early_scales, 0, LAST * P, [nc.sync] * 4)
-        for lo, hi in halves:
-            scale(t, 2, lo, hi)
-            round_y(t, 2, nc.scalar, lo, hi)
-        store_y(t, 2, 3)
-        y_copy(t, 0, nc.vector)
-        y_transposes(t, 1)
-        y_copy(t, 1, nc.scalar)
+        y_quantize(t, 2)
         y_quantize(t, 0)
         y_quantize(t, 1)
-        store_codes(t, 0, 2)
-        y_quantize(t, 2)
-        store_codes(t, 2, 3)
-        store_scales(last_scales, LAST * P, B, [nc.sync, nc.scalar, nc.sync, nc.scalar])
+        store_codes(t, 0, 3)
+        store_scales(last_scales, EARLY * P, B, [nc.sync, nc.scalar] * 2)

@@ -22,7 +22,7 @@ TILES = B // P
 CHUNKS = R // K_PASS
 LAST = TILES - 1
 LOW, HIGH = (0, 1), (2, 3)
-EARLY = TILES - 2
+EARLY = TILES // 2
 
 
 def tile_reservoir_state_step_g4_kernel(
@@ -67,27 +67,27 @@ def tile_reservoir_state_step_g4_kernel(
             for g in range(CHUNKS):
                 w_codes[g, c] = w[:, g, :]
 
-        def load_win():
-            w = keep.tile([P, 2 * R], U8, name="win", align_bytes=64)
-            nc.sync.dma_start(out=w[:].bitcast(I32), in_=win_words[0].bitcast(I32))
-            for c in range(CHUNKS):
-                w_codes[CHUNKS, c] = w[:, c * 1024 : (c + 1) * 1024]
+        def load_win(first, last):
+            w = keep.tile([P, (last - first) * 1024], U8, name="win_%d" % first, align_bytes=64)
+            nc.sync.dma_start(out=w[:].bitcast(I32), in_=win_words[0, :, first * 1024 : last * 1024].bitcast(I32))
+            for c in range(first, last):
+                w_codes[CHUNKS, c] = w[:, (c - first) * 1024 : (c - first + 1) * 1024]
 
         whole = [(h, 0, 0, CHUNKS), (u, CHUNKS, 0, 1)]
         bias_col = load_column("bias_col", bias)
         load_x(0, whole)
-        for q in range(4):
-            src = wr_scales[:, 4 * q : 4 * q + 4, :].rearrange("g r n -> r g n")
-            nc.scalar.dma_start(out=wr_sc[32 * q : 32 * q + 4].bitcast(I32), in_=src.bitcast(I32))
+        for r in range(4):
+            src = wr_scales[:, r::4, :].rearrange("g q n -> q g n")
+            nc.sync.dma_start(out=wr_sc[r:P:32].bitcast(I32), in_=src.bitcast(I32))
         load_wr(0)
-        load_win()
+        load_win(0, 1)
+        for r in range(4):
+            nc.sync.dma_start(out=win_sc[r:P:32].bitcast(I32), in_=win_scales[0, r::4, :].bitcast(I32))
         load_x(1, whole)
-        for q in range(4):
-            src = win_scales[0, 4 * q : 4 * q + 4, :]
-            nc.sync.dma_start(out=win_sc[32 * q : 32 * q + 4].bitcast(I32), in_=src.bitcast(I32))
-        load_wr(1)
-        load_wr(2)
         amp_col = load_column("amp_col", amp)
+        load_wr(1)
+        load_win(1, CHUNKS)
+        load_wr(2)
         for t in range(2, TILES):
             load_x(t, whole)
 
@@ -145,7 +145,7 @@ def tile_reservoir_state_step_g4_kernel(
                         nc.tensor.transpose(bank[:, at : at + P], words[:, c, w : w + 1].to_broadcast([P, P]), ident[:])
                 interleave(nc.scalar, rows[:, part * 1024 : part * 1024 + len(chunks) * K_PASS], bank, len(chunks))
 
-        acc, pre, y_rows, y_bf, y_bank, y_grouped, y_codes = {}, {}, {}, {}, {}, {}, {}
+        acc, pre, y_rows, y_bf, y_bank, y_grouped = {}, {}, {}, {}, {}, {}
 
         def matmuls(t, c):
             bank = psum.tile([P, 512], F32, name="acc", bufs=4)
@@ -184,12 +184,11 @@ def tile_reservoir_state_step_g4_kernel(
             cols = slice(first * K_PASS, last * K_PASS)
             nc.sync.dma_start(out=out_0[t * P : (t + 1) * P, cols], in_=y_rows[t][:, cols])
 
-        def round_y(t, c, engine, lo=0, hi=K_PASS):
-            if lo == 0:
-                y_bf[t, c] = work.tile([P, K_PASS], BF16, name="y_bf", bufs=6)
-            dst = y_bf[t, c][:].rearrange("p (w a b e) -> p a w b e", w=2, b=4, e=2)
-            src = y_rows[t][:, c * K_PASS : (c + 1) * K_PASS].rearrange("p (a b w e) -> p a w b e", b=4, w=2, e=2)
-            copy(engine, dst[:, lo // 16 : hi // 16], src[:, lo // 16 : hi // 16])
+        def round_y(t, c, engine):
+            y_bf[t, c] = work.tile([P, K_PASS], BF16, name="y_bf", bufs=6)
+            dst = y_bf[t, c][:].rearrange("p (w j e) -> p w j e", w=2, e=2)
+            src = y_rows[t][:, c * K_PASS : (c + 1) * K_PASS].rearrange("p (j w e) -> p w j e", w=2, e=2)
+            copy(engine, dst, src)
 
         def scale_round(t, c, lo, hi):
             if lo == 0:
@@ -203,7 +202,7 @@ def tile_reservoir_state_step_g4_kernel(
             )
 
         def y_transposes(t, chunks, name):
-            bank = psum.tile([P, 512], F32, name=name)
+            bank = psum.tile([P, 512], F32, name=name, bufs=4 if name == "acc" else 1)
             for i, c in enumerate(chunks):
                 words = y_bf[t, c][:].bitcast(F32)
                 for w in range(2):
@@ -217,19 +216,18 @@ def tile_reservoir_state_step_g4_kernel(
             for i, c in enumerate(chunks):
                 y_grouped[t, c] = grouped[:, i * K_PASS : (i + 1) * K_PASS]
 
+        y_codes = keep.tile([P, CHUNKS, B], U32, name="y_codes", align_bytes=64)
         early_scales = keep.tile([P, CHUNKS, EARLY * P], U8, name="early_scales", align_bytes=64)
         last_scales = keep.tile([P, CHUNKS, B - EARLY * P], U8, name="last_scales", align_bytes=64)
 
         def y_quantize(t, c):
-            if t not in y_codes:
-                y_codes[t] = work.tile([P, CHUNKS, P], U32, name="y_codes", align_bytes=64)
             plane, at = (early_scales, t * P) if t < EARLY else (last_scales, (t - EARLY) * P)
             scales = plane[:, c, at : at + P]
-            nc.vector.quantize_mx(out=y_codes[t][:, c, :].bitcast(FP8X4), scales=scales, in_=y_grouped[t, c])
+            nc.vector.quantize_mx(out=y_codes[:, c, t * P : (t + 1) * P].bitcast(FP8X4), scales=scales, in_=y_grouped[t, c])
 
-        def store_codes(t, first, last):
-            dst = out_1.rearrange("g p m t -> p g (m t)")[:, first:last, t * 4 * P : (t + 1) * 4 * P]
-            nc.sync.dma_start(out=dst.bitcast(I32), in_=y_codes[t][:, first:last, :].bitcast(I32))
+        def store_codes(first, last, groups=slice(0, CHUNKS)):
+            dst = out_1.rearrange("g p m t -> p g (m t)")[:, groups, first * 4 * P : last * 4 * P]
+            nc.sync.dma_start(out=dst.bitcast(I32), in_=y_codes[:, groups, first * P : last * P].bitcast(I32))
 
         def store_scales(scales, lo, hi, engines):
             for q in range(4):
@@ -247,93 +245,123 @@ def tile_reservoir_state_step_g4_kernel(
                 x_quantize(0, (g - 1,))
                 x_quantize(0, (g,))
 
-        for t in range(TILES):
+        for t in range(LAST):
             more_x = t + 2 < TILES
             matmuls(t, 0)
             if t >= 1:
-                round_y(t - 1, 0, nc.scalar)
                 add_bias(t - 1, 2)
                 tanh(t - 1, 2)
                 scale(t - 1, 1, nc.vector)
+                round_y(t - 1, 0, nc.scalar)
                 round_y(t - 1, 1, nc.scalar)
+            if t >= 3:
+                y_quantize(t - 3, 2)
+                if t % 2 == 0:
+                    store_codes(t - 4, t - 2)
+                if t - 2 == EARLY:
+                    store_scales(early_scales, 0, EARLY * P, [nc.sync] * 4)
+            if t >= 2:
+                y_quantize(t - 2, 0)
+                y_quantize(t - 2, 1)
+            if t >= 1:
+                x_quantize(t + 1, LOW)
+                x_quantize(t + 1, HIGH)
+            if t >= 1:
+                scale(t - 1, 2, nc.gpsimd)
+                store_y(t - 1, 0, CHUNKS)
             add_bias(t, 0)
             if t == 0:
                 x_run(1)
                 spread(amp_col, amp_rows)
             matmuls(t, 1)
-            if t >= 1:
-                scale(t - 1, 2, nc.vector)
-                store_y(t - 1, 0, CHUNKS)
             tanh(t, 0)
+            scale(t, 0, nc.gpsimd)
             if t == 0:
                 x_copy(1, LOW, nc.vector)
                 x_copy(1, HIGH, nc.vector)
             add_bias(t, 1)
-            scale(t, 0, nc.vector)
             if t == 0:
                 x_quantize(1, LOW)
                 x_quantize(1, HIGH)
-            if t >= 1:
-                round_y(t - 1, 2, nc.vector if more_x else nc.scalar)
+            mid_run = 1 <= t and more_x
+            if not mid_run:
+                matmuls(t, 2)
             if more_x:
                 x_run(t + 2)
-            if t >= 1:
-                y_transposes(t - 1, LOW, "y_bank_0")
             if t >= 2:
                 y_transposes(t - 2, (2,), "y_bank_1")
-            matmuls(t, 2)
+            if t >= 1:
+                y_transposes(t - 1, LOW, "y_bank_0")
+            if mid_run:
+                matmuls(t, 2)
             if more_x:
                 x_copy(t + 2, LOW, nc.scalar)
-            if t == LAST:
-                y_copy(t - 2, (2,), nc.scalar)
             tanh(t, 1)
             if more_x:
-                x_quantize(t + 2, LOW)
                 x_copy(t + 2, HIGH, nc.scalar)
-            if t >= 2:
-                y_quantize(t - 2, 0)
-                y_quantize(t - 2, 1)
-            if t >= 3:
-                y_quantize(t - 3, 2)
-                store_codes(t - 3, 0, CHUNKS)
-            if more_x:
-                x_quantize(t + 2, HIGH)
-            if 1 <= t < LAST:
-                y_copy(t - 1, LOW, nc.scalar)
-            if 2 <= t < LAST:
-                y_copy(t - 2, (2,), nc.scalar)
-        y_quantize(LAST - 2, 2)
-        store_codes(LAST - 2, 0, CHUNKS)
-        store_scales(early_scales, 0, EARLY * P, [nc.sync] * 4)
+            if t >= 1:
+                round_y(t - 1, 2, nc.scalar)
+            if t >= 2 and more_x:
+                y_copy(t - 2, (2,), nc.vector)
+            if t >= 1 and more_x:
+                y_copy(t - 1, LOW, nc.vector)
 
         t = LAST
         halves = ((0, 256), (256, 512))
-        round_y(t, 0, nc.scalar)
+        matmuls(t, 0)
+        add_bias(t - 1, 2)
+        matmuls(t, 1)
+        y_copy(t - 3, (2,), nc.vector)
+        y_copy(t - 2, LOW, nc.vector)
+        tanh(t - 1, 2)
+        scale(t - 1, 1, nc.vector)
+        scale(t - 1, 2, nc.gpsimd)
+        store_y(t - 1, 0, CHUNKS)
+        round_y(t - 1, 0, nc.scalar)
+        round_y(t - 1, 1, nc.scalar)
+        add_bias(t, 0)
+        matmuls(t, 2)
+        add_bias(t, 1)
+        y_transposes(t - 2, (2,), "y_bank_1")
+        y_transposes(t - 1, LOW, "y_bank_0")
+        tanh(t, 0)
+        tanh(t, 1)
+        y_quantize(t - 3, 2)
+        store_codes(t - 3, t - 2)
+        y_quantize(t - 2, 0)
+        y_quantize(t - 2, 1)
+        round_y(t - 1, 2, nc.scalar)
         y_transposes(t - 1, (2,), "x_bank_0")
-        y_transposes(t, (0,), "x_bank_1")
         for lo, hi in halves:
             add_bias(t, 2, lo, hi)
             tanh(t, 2, lo, hi)
+        scale(t, 0, nc.vector)
+        store_y(t, 0, 1)
         scale(t, 1, nc.vector)
-        store_y(t, 0, 2)
+        store_y(t, 1, 2)
+        round_y(t, 0, nc.scalar)
+        y_transposes(t, (0,), "x_bank_1")
         round_y(t, 1, nc.scalar)
+        y_transposes(t, (1,), "acc")
         for lo, hi in halves:
             scale_round(t, 2, lo, hi)
-        y_transposes(t, (2,), "y_bank_1")
-        y_copy(t - 1, LOW, nc.scalar)
-        y_transposes(t, (1,), "y_bank_0")
+        y_transposes(t, (2,), "acc")
         scale(t, 2, nc.vector)
         store_y(t, 2, 3)
-        y_copy(t - 1, (2,), nc.vector)
-        y_copy(t, (2,), nc.scalar)
+        y_copy(t - 1, LOW, nc.scalar)
+        y_copy(t - 2, (2,), nc.vector)
         y_copy(t, (0,), nc.vector)
+        y_copy(t, (1,), nc.scalar)
+        y_quantize(t - 2, 2)
+        store_codes(t - 2, t - 1)
+        y_copy(t - 1, (2,), nc.scalar)
         y_quantize(t - 1, 0)
         y_quantize(t - 1, 1)
-        y_copy(t, (1,), nc.scalar)
-        y_quantize(t - 1, 2)
-        store_codes(t - 1, 0, CHUNKS)
-        y_quantize(t, 2)
+        y_copy(t, (2,), nc.scalar)
         y_quantize(t, 0)
         y_quantize(t, 1)
-        store_codes(t, 0, 3)
+        store_codes(t - 1, t + 1, slice(0, 2))
+        y_quantize(t - 1, 2)
+        y_quantize(t, 2)
+        store_codes(t - 1, t + 1, slice(2, 3))
         store_scales(last_scales, EARLY * P, B, [nc.sync, nc.scalar] * 2)

@@ -43,18 +43,20 @@ def tile_reservoir_state_step_g4_kernel(
         nc.vector.memset(wr_sc[:].bitcast(I32), 0)
         nc.vector.memset(win_sc[:].bitcast(I32), 0)
 
-        def load_column(label, vec):
+        def load_column(label, vec, engine):
             col = keep.tile([P, CHUNKS, 4], BF16, name=label)
-            nc.sync.dma_start(out=col[:], in_=vec.rearrange("(c p e) -> p c e", c=CHUNKS, e=4))
+            engine.dma_start(out=col[:], in_=vec.rearrange("(c p e) -> p c e", c=CHUNKS, e=4))
             return col
 
-        x_raw = {}
+        x_raw, x_rows = {}, {}
 
         def load_x(t, spans):
             rows = slice(t * P, (t + 1) * P)
             for src, g0, first, count in spans:
                 raw = keep.tile([P, count * K_PASS], BF16, name="x_raw_%d_%d" % (t, g0))
                 nc.sync.dma_start(out=raw[:], in_=src[rows, first * K_PASS : (first + count) * K_PASS])
+                if g0 == 0:
+                    x_rows[t] = raw
                 for i in range(count):
                     x_raw[t, g0 + i] = raw[:].bitcast(F32)[:, i * 256 : (i + 1) * 256]
 
@@ -74,7 +76,7 @@ def tile_reservoir_state_step_g4_kernel(
                 w_codes[CHUNKS, c] = w[:, (c - first) * 1024 : (c - first + 1) * 1024]
 
         whole = [(h, 0, 0, CHUNKS), (u, CHUNKS, 0, 1)]
-        bias_col = load_column("bias_col", bias)
+        bias_col = load_column("bias_col", bias, nc.scalar)
         load_x(0, whole)
         for r in range(4):
             src = wr_scales[:, r::4, :].rearrange("g q n -> q g n")
@@ -84,7 +86,7 @@ def tile_reservoir_state_step_g4_kernel(
         for r in range(4):
             nc.sync.dma_start(out=win_sc[r:P:32].bitcast(I32), in_=win_scales[0, r::4, :].bitcast(I32))
         load_x(1, whole)
-        amp_col = load_column("amp_col", amp)
+        amp_col = load_column("amp_col", amp, nc.sync)
         load_wr(1)
         load_win(1, CHUNKS)
         load_wr(2)
@@ -110,12 +112,23 @@ def tile_reservoir_state_step_g4_kernel(
 
         x_bank, x_grouped, x_codes, x_scales = {}, {}, {}, {}
 
+        x_sorted = {}
+
+        def x_sort(t):
+            count = 2
+            ordered = work.tile([P, count, 2, P], F32, name="x_sorted", bufs=3)
+            src = x_rows[t][:].bitcast(F32)[:, : count * 256].rearrange("p (g j w) -> p g w j", g=count, w=2)
+            nc.vector.tensor_copy(out=ordered[:], in_=src)
+            for g in range(count):
+                x_sorted[t, g] = ordered[:, g]
+
         def x_transposes(t, passes, name):
             bank = psum.tile([P, 512], F32, name=name, bufs=4 if name == "acc" else 1)
             for i, g in enumerate(passes):
                 for w in range(2):
                     at = (2 * i + w) * P
-                    nc.tensor.transpose(bank[:, at : at + P], x_raw[t, g][:, w::2], ident[:])
+                    words = x_sorted[t, g][:, w, :] if (t, g) in x_sorted else x_raw[t, g][:, w::2]
+                    nc.tensor.transpose(bank[:, at : at + P], words, ident[:])
             x_bank[t, passes] = bank
 
         def x_copy(t, passes, engine):
@@ -132,8 +145,8 @@ def tile_reservoir_state_step_g4_kernel(
                 x_scales[t, g] = scales[:, i * P : (i + 1) * P]
 
         def x_run(t):
-            x_transposes(t, LOW, "x_bank_0")
             x_transposes(t, HIGH, "x_bank_1")
+            x_transposes(t, LOW, "x_bank_0")
 
         def spread(col, rows):
             words = col[:].bitcast(F32)
@@ -251,6 +264,8 @@ def tile_reservoir_state_step_g4_kernel(
             if t >= 1:
                 add_bias(t - 1, 2)
                 tanh(t - 1, 2)
+                if t == 1:
+                    x_sort(3)
                 scale(t - 1, 1, nc.vector)
                 round_y(t - 1, 0, nc.scalar)
                 round_y(t - 1, 1, nc.scalar)
@@ -264,8 +279,10 @@ def tile_reservoir_state_step_g4_kernel(
                 y_quantize(t - 2, 0)
                 y_quantize(t - 2, 1)
             if t >= 1:
-                x_quantize(t + 1, LOW)
                 x_quantize(t + 1, HIGH)
+                x_quantize(t + 1, LOW)
+                if t + 3 < TILES:
+                    x_sort(t + 3)
             if t >= 1:
                 scale(t - 1, 2, nc.gpsimd)
                 store_y(t - 1, 0, CHUNKS)
@@ -277,12 +294,11 @@ def tile_reservoir_state_step_g4_kernel(
             tanh(t, 0)
             scale(t, 0, nc.gpsimd)
             if t == 0:
-                x_copy(1, LOW, nc.vector)
                 x_copy(1, HIGH, nc.vector)
-            add_bias(t, 1)
-            if t == 0:
-                x_quantize(1, LOW)
+                x_copy(1, LOW, nc.vector)
                 x_quantize(1, HIGH)
+                x_quantize(1, LOW)
+            add_bias(t, 1)
             mid_run = 1 <= t and more_x
             if not mid_run:
                 matmuls(t, 2)
@@ -295,10 +311,10 @@ def tile_reservoir_state_step_g4_kernel(
             if mid_run:
                 matmuls(t, 2)
             if more_x:
-                x_copy(t + 2, LOW, nc.scalar)
+                x_copy(t + 2, HIGH, nc.scalar)
             tanh(t, 1)
             if more_x:
-                x_copy(t + 2, HIGH, nc.scalar)
+                x_copy(t + 2, LOW, nc.scalar)
             if t >= 1:
                 round_y(t - 1, 2, nc.scalar)
             if t >= 2 and more_x:

@@ -18,10 +18,15 @@ ACT = mybir.ActivationFunctionType
 
 P = 128
 K_PASS = 512
+CHUNK = 512
+PAIRS = K_PASS // 2
+W_BYTES = 2 * CHUNK
 TILES = B // P
-CHUNKS = R // K_PASS
-LAST = TILES - 1
+CHUNKS = R // CHUNK
+H_PASSES = R // K_PASS
 LOW, HIGH = (0, 1), (2, 3)
+ALL = LOW + HIGH
+ACC_BANKS = 4
 EARLY = TILES // 2
 
 
@@ -29,6 +34,7 @@ def tile_reservoir_state_step_g4_kernel(
     tc, h, u, wr_words, wr_scales, win_words, win_scales, bias, amp, out_0, out_1, out_2
 ):
     nc = tc.nc
+    V, S, G = nc.vector, nc.scalar, nc.gpsimd
     with ExitStack() as ctx:
         keep = ctx.enter_context(tc.tile_pool(name="keep", bufs=1))
         work = ctx.enter_context(tc.tile_pool(name="work", bufs=4))
@@ -38,46 +44,44 @@ def tile_reservoir_state_step_g4_kernel(
         ident = keep.tile([P, P], F32, name="ident")
         make_identity(nc, ident[:])
 
-        wr_sc = keep.tile([P, CHUNKS, R], U8, name="wr_sc", align_bytes=64)
+        wr_sc = keep.tile([P, H_PASSES, R], U8, name="wr_sc", align_bytes=64)
         win_sc = keep.tile([P, R], U8, name="win_sc", align_bytes=64)
-        nc.vector.memset(wr_sc[:].bitcast(I32), 0)
-        nc.vector.memset(win_sc[:].bitcast(I32), 0)
+        V.memset(wr_sc[:].bitcast(I32), 0)
+        V.memset(win_sc[:].bitcast(I32), 0)
 
-        def load_column(label, vec, engine):
-            col = keep.tile([P, CHUNKS, 4], BF16, name=label)
-            engine.dma_start(out=col[:], in_=vec.rearrange("(c p e) -> p c e", c=CHUNKS, e=4))
+        h_rows, x_pairs, w_codes = {}, {}, {}
+
+        def load_column(name, vec):
+            col = keep.tile([P, CHUNKS, 4], BF16, name=name)
+            nc.sync.dma_start(out=col[:], in_=vec.rearrange("(c p j) -> p c j", c=CHUNKS, j=4))
             return col
 
-        x_raw, x_rows = {}, {}
-
-        def load_x(t, spans):
+        def load_x(t):
             rows = slice(t * P, (t + 1) * P)
-            for src, g0, first, count in spans:
-                raw = keep.tile([P, count * K_PASS], BF16, name="x_raw_%d_%d" % (t, g0))
-                nc.sync.dma_start(out=raw[:], in_=src[rows, first * K_PASS : (first + count) * K_PASS])
-                if g0 == 0:
-                    x_rows[t] = raw
-                for i in range(count):
-                    x_raw[t, g0 + i] = raw[:].bitcast(F32)[:, i * 256 : (i + 1) * 256]
-
-        w_codes = {}
+            h_rows[t] = keep.tile([P, R], BF16, name="h_rows_%d" % t)
+            nc.sync.dma_start(out=h_rows[t][:], in_=h[rows, :])
+            u_rows = keep.tile([P, U], BF16, name="u_rows_%d" % t)
+            nc.sync.dma_start(out=u_rows[:], in_=u[rows, :])
+            for g in range(H_PASSES):
+                x_pairs[t, g] = h_rows[t][:].bitcast(F32)[:, g * PAIRS : (g + 1) * PAIRS]
+            x_pairs[t, H_PASSES] = u_rows[:].bitcast(F32)
 
         def load_wr(c):
-            w = keep.tile([P, CHUNKS, 1024], U8, name="wr_%d" % c, align_bytes=64)
-            src = wr_words[:, :, c * 1024 : (c + 1) * 1024].rearrange("g p n -> p g n")
-            nc.sync.dma_start(out=w[:].bitcast(I32), in_=src.bitcast(I32))
-            for g in range(CHUNKS):
-                w_codes[g, c] = w[:, g, :]
+            codes = keep.tile([P, H_PASSES, W_BYTES], U8, name="wr_%d" % c, align_bytes=64)
+            src = wr_words[:, :, c * W_BYTES : (c + 1) * W_BYTES].rearrange("g p n -> p g n")
+            nc.sync.dma_start(out=codes[:].bitcast(I32), in_=src.bitcast(I32))
+            for g in range(H_PASSES):
+                w_codes[g, c] = codes[:, g, :]
 
         def load_win(first, last):
-            w = keep.tile([P, (last - first) * 1024], U8, name="win_%d" % first, align_bytes=64)
-            nc.sync.dma_start(out=w[:].bitcast(I32), in_=win_words[0, :, first * 1024 : last * 1024].bitcast(I32))
+            codes = keep.tile([P, (last - first) * W_BYTES], U8, name="win_%d" % first, align_bytes=64)
+            src = win_words[0, :, first * W_BYTES : last * W_BYTES]
+            nc.sync.dma_start(out=codes[:].bitcast(I32), in_=src.bitcast(I32))
             for c in range(first, last):
-                w_codes[CHUNKS, c] = w[:, (c - first) * 1024 : (c - first + 1) * 1024]
+                w_codes[H_PASSES, c] = codes[:, (c - first) * W_BYTES : (c - first + 1) * W_BYTES]
 
-        whole = [(h, 0, 0, CHUNKS), (u, CHUNKS, 0, 1)]
-        bias_col = load_column("bias_col", bias, nc.scalar)
-        load_x(0, whole)
+        bias_col = load_column("bias_col", bias)
+        load_x(0)
         for r in range(4):
             src = wr_scales[:, r::4, :].rearrange("g q n -> q g n")
             nc.sync.dma_start(out=wr_sc[r:P:32].bitcast(I32), in_=src.bitcast(I32))
@@ -85,299 +89,318 @@ def tile_reservoir_state_step_g4_kernel(
         load_win(0, 1)
         for r in range(4):
             nc.sync.dma_start(out=win_sc[r:P:32].bitcast(I32), in_=win_scales[0, r::4, :].bitcast(I32))
-        load_x(1, whole)
-        amp_col = load_column("amp_col", amp, nc.sync)
+        load_x(1)
+        amp_col = load_column("amp_col", amp)
         load_wr(1)
         load_win(1, CHUNKS)
         load_wr(2)
         for t in range(2, TILES):
-            load_x(t, whole)
+            load_x(t)
 
-        def w_scale(g, c):
-            cols = slice(c * K_PASS, (c + 1) * K_PASS)
-            return wr_sc[:, g, cols] if g < CHUNKS else win_sc[:, cols]
+        def bank_tile(name):
+            return psum.tile([P, 512], F32, name=name, bufs=ACC_BANKS if name == "acc" else 1)
 
         def copy(engine, out, in_):
-            if engine is nc.scalar:
-                nc.scalar.copy(out=out, in_=in_)
+            if engine is S:
+                S.copy(out=out, in_=in_)
             else:
-                nc.vector.tensor_copy(out=out, in_=in_)
+                V.tensor_copy(out=out, in_=in_)
 
         def interleave(engine, dst, bank, groups):
             copy(
                 engine,
-                dst.bitcast(F32).rearrange("p (g r u) -> p g r u", g=groups, u=2),
-                bank[:, : groups * 256].rearrange("p (g u r) -> p g r u", g=groups, u=2),
+                dst.bitcast(F32).rearrange("p (g m w) -> p g m w", g=groups, w=2),
+                bank[:, : groups * 2 * P].rearrange("p (g w m) -> p g m w", g=groups, w=2),
             )
 
-        x_bank, x_grouped, x_codes, x_scales = {}, {}, {}, {}
+        def spread(col, rows):
+            pairs = col[:].bitcast(F32)
+            for name, chunks in (("y_bank_0", LOW), ("y_bank_1", (2,))):
+                bank = bank_tile(name)
+                for i, c in enumerate(chunks):
+                    for w in range(2):
+                        at = (2 * i + w) * P
+                        repeated = pairs[:, c, w : w + 1].to_broadcast([P, P])
+                        nc.tensor.transpose(bank[:, at : at + P], repeated, ident[:])
+                interleave(S, rows[:, chunks[0] * CHUNK : (chunks[-1] + 1) * CHUNK], bank, len(chunks))
 
-        x_sorted = {}
+        x_sorted, x_bank, x_grouped, x_codes, x_scales = {}, {}, {}, {}, {}
 
-        def x_sort(t):
-            count = 2
+        def x_sort(t, count):
             ordered = work.tile([P, count, 2, P], F32, name="x_sorted", bufs=3)
-            src = x_rows[t][:].bitcast(F32)[:, : count * 256].rearrange("p (g j w) -> p g w j", g=count, w=2)
-            nc.vector.tensor_copy(out=ordered[:], in_=src)
+            src = h_rows[t][:].bitcast(F32)[:, : count * PAIRS].rearrange("p (g j w) -> p g w j", g=count, w=2)
+            V.tensor_copy(out=ordered[:], in_=src)
             for g in range(count):
                 x_sorted[t, g] = ordered[:, g]
 
         def x_transposes(t, passes, name):
-            bank = psum.tile([P, 512], F32, name=name, bufs=4 if name == "acc" else 1)
+            bank = bank_tile(name)
             for i, g in enumerate(passes):
                 for w in range(2):
                     at = (2 * i + w) * P
-                    words = x_sorted[t, g][:, w, :] if (t, g) in x_sorted else x_raw[t, g][:, w::2]
-                    nc.tensor.transpose(bank[:, at : at + P], words, ident[:])
+                    pairs = x_sorted[t, g][:, w, :] if (t, g) in x_sorted else x_pairs[t, g][:, w::2]
+                    nc.tensor.transpose(bank[:, at : at + P], pairs, ident[:])
             x_bank[t, passes] = bank
 
-        def x_copy(t, passes, engine):
-            grouped = work.tile([P, len(passes) * K_PASS], BF16, name="x_grouped", align_bytes=64)
-            interleave(engine, grouped[:], x_bank[t, passes], len(passes))
-            x_grouped[t, passes] = grouped
+        def x_run(t):
+            x_transposes(t, LOW, "x_bank_0")
+            x_transposes(t, HIGH, "x_bank_1")
 
-        def x_quantize(t, passes):
-            codes = work.tile([P, len(passes) * P], U32, name="x_codes", align_bytes=64, bufs=8)
-            scales = work.tile([P, len(passes) * P], U8, name="x_scales", align_bytes=64, bufs=8)
-            nc.vector.quantize_mx(out=codes[:].bitcast(FP8X4), scales=scales[:], in_=x_grouped[t, passes][:])
+        def x_copy(t, passes, engine, together=ALL):
+            if (t, together) not in x_grouped:
+                x_grouped[t, together] = work.tile([P, len(together) * K_PASS], BF16, name="x_grouped", align_bytes=64)
+            at = (passes[0] - together[0]) * K_PASS
+            dst = x_grouped[t, together][:, at : at + len(passes) * K_PASS]
+            interleave(engine, dst, x_bank[t, passes], len(passes))
+
+        def x_quantize(t, passes=ALL):
+            codes = work.tile([P, len(passes) * P], U32, name="x_codes", align_bytes=64, bufs=6)
+            scales = work.tile([P, len(passes) * P], U8, name="x_scales", align_bytes=64, bufs=6)
+            V.quantize_mx(out=codes[:].bitcast(FP8X4), scales=scales[:], in_=x_grouped[t, passes][:])
             for i, g in enumerate(passes):
                 x_codes[t, g] = codes[:, i * P : (i + 1) * P]
                 x_scales[t, g] = scales[:, i * P : (i + 1) * P]
 
-        def x_run(t):
-            x_transposes(t, HIGH, "x_bank_1")
-            x_transposes(t, LOW, "x_bank_0")
-
-        def spread(col, rows):
-            words = col[:].bitcast(F32)
-            for part, chunks in enumerate(((0, 1), (2,))):
-                bank = psum.tile([P, 512], F32, name="y_bank_%d" % part)
-                for i, c in enumerate(chunks):
-                    for w in range(2):
-                        at = (2 * i + w) * P
-                        nc.tensor.transpose(bank[:, at : at + P], words[:, c, w : w + 1].to_broadcast([P, P]), ident[:])
-                interleave(nc.scalar, rows[:, part * 1024 : part * 1024 + len(chunks) * K_PASS], bank, len(chunks))
-
         acc, pre, y_rows, y_bf, y_bank, y_grouped = {}, {}, {}, {}, {}, {}
 
         def matmuls(t, c):
-            bank = psum.tile([P, 512], F32, name="acc", bufs=4)
-            for g in range(CHUNKS + 1):
+            cols = slice(c * CHUNK, (c + 1) * CHUNK)
+            acc[t, c] = bank_tile("acc")
+            for g in ALL:
                 nc.tensor.matmul_mx(
-                    out=bank[:],
+                    out=acc[t, c][:],
                     lhsT=x_codes[t, g].bitcast(FP8X4),
                     lhsT_scale=x_scales[t, g],
                     rhs=w_codes[g, c].bitcast(FP4X4),
-                    rhs_scale=w_scale(g, c),
-                    start=(g == 0),
-                    stop=(g == CHUNKS),
+                    rhs_scale=wr_sc[:, g, cols] if g < H_PASSES else win_sc[:, cols],
+                    start=(g == ALL[0]),
+                    stop=(g == ALL[-1]),
                 )
-            acc[t, c] = bank
 
-        def add_bias(t, c, lo=0, hi=K_PASS):
+        def add_bias(t, c, lo=0, hi=CHUNK):
             if lo == 0:
-                pre[t, c] = work.tile([P, K_PASS], F32, name="pre")
-            nc.vector.tensor_tensor(
+                pre[t, c] = work.tile([P, CHUNK], F32, name="pre")
+            V.tensor_tensor(
                 out=pre[t, c][:, lo:hi],
                 in0=acc[t, c][:, lo:hi],
-                in1=bias_rows[:, c * K_PASS + lo : c * K_PASS + hi],
+                in1=bias_rows[:, c * CHUNK + lo : c * CHUNK + hi],
                 op=ALU.add,
             )
 
-        def tanh(t, c, lo=0, hi=K_PASS):
-            nc.scalar.activation(out=pre[t, c][:, lo:hi], in_=pre[t, c][:, lo:hi], func=ACT.Tanh)
+        def tanh(t, c, lo=0, hi=CHUNK):
+            S.activation(out=pre[t, c][:, lo:hi], in_=pre[t, c][:, lo:hi], func=ACT.Tanh)
 
-        def scale(t, c, engine, lo=0, hi=K_PASS):
-            if (t, c, lo) == (t, 0, 0):
+        def scale(t, c, engine):
+            if c == 0:
                 y_rows[t] = work.tile([P, R], F32, name="y_rows")
-            cols = slice(c * K_PASS + lo, c * K_PASS + hi)
-            engine.tensor_tensor(out=y_rows[t][:, cols], in0=pre[t, c][:, lo:hi], in1=amp_rows[:, cols], op=ALU.mult)
+            cols = slice(c * CHUNK, (c + 1) * CHUNK)
+            engine.tensor_tensor(out=y_rows[t][:, cols], in0=pre[t, c][:], in1=amp_rows[:, cols], op=ALU.mult)
 
         def store_y(t, first, last):
-            cols = slice(first * K_PASS, last * K_PASS)
+            cols = slice(first * CHUNK, last * CHUNK)
             nc.sync.dma_start(out=out_0[t * P : (t + 1) * P, cols], in_=y_rows[t][:, cols])
 
-        def round_y(t, c, engine):
-            y_bf[t, c] = work.tile([P, K_PASS], BF16, name="y_bf", bufs=6)
-            dst = y_bf[t, c][:].rearrange("p (w j e) -> p w j e", w=2, e=2)
-            src = y_rows[t][:, c * K_PASS : (c + 1) * K_PASS].rearrange("p (j w e) -> p w j e", w=2, e=2)
-            copy(engine, dst, src)
+        def by_pair(values):
+            return values.rearrange("p (j w e) -> p w j e", w=2, e=2)
+
+        def rounded_tile(t, c):
+            y_bf[t, c] = work.tile([P, CHUNK], BF16, name="y_bf", bufs=6)
+
+        def rounded_view(t, c):
+            return y_bf[t, c][:].rearrange("p (w j e) -> p w j e", w=2, e=2)
+
+        def round_y(t, c):
+            rounded_tile(t, c)
+            S.copy(out=rounded_view(t, c), in_=by_pair(y_rows[t][:, c * CHUNK : (c + 1) * CHUNK]))
 
         def scale_round(t, c, lo, hi):
             if lo == 0:
-                y_bf[t, c] = work.tile([P, K_PASS], BF16, name="y_bf", bufs=6)
-            words = slice(lo // 4, hi // 4)
-            nc.vector.tensor_tensor(
-                out=y_bf[t, c][:].rearrange("p (w j e) -> p w j e", w=2, e=2)[:, :, words],
-                in0=pre[t, c][:].rearrange("p (j w e) -> p w j e", w=2, e=2)[:, :, words],
-                in1=amp_rows[:, c * K_PASS : (c + 1) * K_PASS].rearrange("p (j w e) -> p w j e", w=2, e=2)[:, :, words],
+                rounded_tile(t, c)
+            js = slice(lo // 4, hi // 4)
+            V.tensor_tensor(
+                out=rounded_view(t, c)[:, :, js],
+                in0=by_pair(pre[t, c][:])[:, :, js],
+                in1=by_pair(amp_rows[:, c * CHUNK : (c + 1) * CHUNK])[:, :, js],
                 op=ALU.mult,
             )
 
         def y_transposes(t, chunks, name):
-            bank = psum.tile([P, 512], F32, name=name, bufs=4 if name == "acc" else 1)
+            bank = bank_tile(name)
             for i, c in enumerate(chunks):
-                words = y_bf[t, c][:].bitcast(F32)
+                pairs = y_bf[t, c][:].bitcast(F32)
                 for w in range(2):
                     at = (2 * i + w) * P
-                    nc.tensor.transpose(bank[:, at : at + P], words[:, w * P : (w + 1) * P], ident[:])
+                    nc.tensor.transpose(bank[:, at : at + P], pairs[:, w * P : (w + 1) * P], ident[:])
             y_bank[t, chunks] = bank
 
         def y_copy(t, chunks, engine):
-            grouped = work.tile([P, len(chunks) * K_PASS], BF16, name="y_grouped", align_bytes=64, bufs=6)
+            grouped = work.tile([P, len(chunks) * CHUNK], BF16, name="y_grouped", align_bytes=64, bufs=8)
             interleave(engine, grouped[:], y_bank[t, chunks], len(chunks))
             for i, c in enumerate(chunks):
-                y_grouped[t, c] = grouped[:, i * K_PASS : (i + 1) * K_PASS]
+                y_grouped[t, c] = grouped[:, i * CHUNK : (i + 1) * CHUNK]
 
         y_codes = keep.tile([P, CHUNKS, B], U32, name="y_codes", align_bytes=64)
         early_scales = keep.tile([P, CHUNKS, EARLY * P], U8, name="early_scales", align_bytes=64)
         last_scales = keep.tile([P, CHUNKS, B - EARLY * P], U8, name="last_scales", align_bytes=64)
 
         def y_quantize(t, c):
-            plane, at = (early_scales, t * P) if t < EARLY else (last_scales, (t - EARLY) * P)
-            scales = plane[:, c, at : at + P]
-            nc.vector.quantize_mx(out=y_codes[:, c, t * P : (t + 1) * P].bitcast(FP8X4), scales=scales, in_=y_grouped[t, c])
+            scales, at = (early_scales, t * P) if t < EARLY else (last_scales, (t - EARLY) * P)
+            V.quantize_mx(
+                out=y_codes[:, c, t * P : (t + 1) * P].bitcast(FP8X4),
+                scales=scales[:, c, at : at + P],
+                in_=y_grouped[t, c],
+            )
 
-        def store_codes(first, last, groups=slice(0, CHUNKS)):
-            dst = out_1.rearrange("g p m t -> p g (m t)")[:, groups, first * 4 * P : last * 4 * P]
-            nc.sync.dma_start(out=dst.bitcast(I32), in_=y_codes[:, groups, first * P : last * P].bitcast(I32))
+        def store_codes(first, last, chunks=slice(0, CHUNKS)):
+            dst = out_1.rearrange("g p m j -> p g (m j)")[:, chunks, first * 4 * P : last * 4 * P]
+            nc.sync.dma_start(out=dst.bitcast(I32), in_=y_codes[:, chunks, first * P : last * P].bitcast(I32))
 
-        def store_scales(scales, lo, hi, engines):
-            for q in range(4):
-                dst = out_2[:, 4 * q : 4 * q + 4, lo:hi].rearrange("g r m -> r g m")
-                engines[q].dma_start(out=dst.bitcast(I32), in_=scales[32 * q : 32 * q + 4].bitcast(I32))
+        def store_scales(scales, lo, hi, queues):
+            for a in range(4):
+                dst = out_2[:, 4 * a : 4 * a + 4, lo:hi].rearrange("g r m -> r g m")
+                queues[a].dma_start(out=dst.bitcast(I32), in_=scales[32 * a : 32 * a + 4].bitcast(I32))
 
         bias_rows = keep.tile([P, R], BF16, name="bias_rows")
         amp_rows = keep.tile([P, R], BF16, name="amp_rows")
         spread(bias_col, bias_rows)
-        for g, name in enumerate(("x_bank_0", "x_bank_1", "acc", "acc")):
+        for g, name in zip(ALL, ("x_bank_0", "x_bank_1", "acc", "acc")):
             x_transposes(0, (g,), name)
-        for g in range(CHUNKS + 1):
-            x_copy(0, (g,), nc.vector if g % 2 == 0 else nc.scalar)
-            if g % 2 == 1:
-                x_quantize(0, (g - 1,))
-                x_quantize(0, (g,))
+        for first, second in (LOW, HIGH):
+            x_copy(0, (first,), V, (first,))
+            x_copy(0, (second,), S, (second,))
+            x_quantize(0, (first,))
+            x_quantize(0, (second,))
 
-        for t in range(LAST):
-            more_x = t + 2 < TILES
+        for t in range(TILES - 2):
             matmuls(t, 0)
             if t >= 1:
+                scale(t - 1, 1, G)
                 add_bias(t - 1, 2)
-                tanh(t - 1, 2)
                 if t == 1:
-                    x_sort(3)
-                scale(t - 1, 1, nc.vector)
-                round_y(t - 1, 0, nc.scalar)
-                round_y(t - 1, 1, nc.scalar)
-            if t >= 3:
-                y_quantize(t - 3, 2)
-                if t % 2 == 0:
-                    store_codes(t - 4, t - 2)
-                if t - 2 == EARLY:
-                    store_scales(early_scales, 0, EARLY * P, [nc.sync] * 4)
-            if t >= 2:
-                y_quantize(t - 2, 0)
-                y_quantize(t - 2, 1)
-            if t >= 1:
-                x_quantize(t + 1, HIGH)
-                x_quantize(t + 1, LOW)
-                if t + 3 < TILES:
-                    x_sort(t + 3)
-            if t >= 1:
-                scale(t - 1, 2, nc.gpsimd)
-                store_y(t - 1, 0, CHUNKS)
+                    x_sort(3, H_PASSES)
+                round_y(t - 1, 0)
+                tanh(t - 1, 2)
+                round_y(t - 1, 1)
             add_bias(t, 0)
             if t == 0:
                 x_run(1)
                 spread(amp_col, amp_rows)
             matmuls(t, 1)
             tanh(t, 0)
-            scale(t, 0, nc.gpsimd)
             if t == 0:
-                x_copy(1, HIGH, nc.vector)
-                x_copy(1, LOW, nc.vector)
-                x_quantize(1, HIGH)
-                x_quantize(1, LOW)
+                x_copy(1, LOW, V)
+                x_copy(1, HIGH, V)
+                x_quantize(1)
+            if t >= 3:
+                y_quantize(t - 3, 2)
+                if t % 2 == 0:
+                    store_codes(t - 4, t - 2)
+            if t >= 2:
+                y_quantize(t - 2, 0)
+                y_quantize(t - 2, 1)
+            if t >= 1:
+                x_quantize(t + 1)
+                if t + 3 < TILES:
+                    x_sort(t + 3, H_PASSES if t == 1 else 1)
+                scale(t - 1, 2, G)
+                store_y(t - 1, 0, CHUNKS)
             add_bias(t, 1)
-            mid_run = 1 <= t and more_x
-            if not mid_run:
+            if t == 0:
                 matmuls(t, 2)
-            if more_x:
-                x_run(t + 2)
+            x_run(t + 2)
             if t >= 2:
                 y_transposes(t - 2, (2,), "y_bank_1")
             if t >= 1:
                 y_transposes(t - 1, LOW, "y_bank_0")
-            if mid_run:
                 matmuls(t, 2)
-            if more_x:
-                x_copy(t + 2, HIGH, nc.scalar)
-            tanh(t, 1)
-            if more_x:
-                x_copy(t + 2, LOW, nc.scalar)
+            if t == 0:
+                tanh(t, 1)
+            x_copy(t + 2, LOW, S)
             if t >= 1:
-                round_y(t - 1, 2, nc.scalar)
-            if t >= 2 and more_x:
-                y_copy(t - 2, (2,), nc.vector)
-            if t >= 1 and more_x:
-                y_copy(t - 1, LOW, nc.vector)
+                tanh(t, 1)
+            x_copy(t + 2, HIGH, S)
+            if t >= 2:
+                y_copy(t - 2, (2,), V)
+            if t >= 1:
+                y_copy(t - 1, LOW, V)
+            scale(t, 0, V)
+            if t >= 1:
+                round_y(t - 1, 2)
 
-        t = LAST
-        halves = ((0, 256), (256, 512))
-        matmuls(t, 0)
-        add_bias(t - 1, 2)
-        matmuls(t, 1)
-        y_copy(t - 3, (2,), nc.vector)
-        y_copy(t - 2, LOW, nc.vector)
-        tanh(t - 1, 2)
-        scale(t - 1, 1, nc.vector)
-        scale(t - 1, 2, nc.gpsimd)
-        store_y(t - 1, 0, CHUNKS)
-        round_y(t - 1, 0, nc.scalar)
-        round_y(t - 1, 1, nc.scalar)
-        add_bias(t, 0)
-        matmuls(t, 2)
-        add_bias(t, 1)
-        y_transposes(t - 2, (2,), "y_bank_1")
-        y_transposes(t - 1, LOW, "y_bank_0")
-        tanh(t, 0)
-        tanh(t, 1)
-        y_quantize(t - 3, 2)
-        store_codes(t - 3, t - 2)
-        y_quantize(t - 2, 0)
-        y_quantize(t - 2, 1)
-        round_y(t - 1, 2, nc.scalar)
-        y_transposes(t - 1, (2,), "x_bank_0")
+        matmuls(6, 0)
+        add_bias(5, 2)
+        tanh(5, 2)
+        scale(5, 1, V)
+        round_y(5, 0)
+        matmuls(6, 1)
+        add_bias(6, 0)
+        round_y(5, 1)
+        x_quantize(7)
+        y_quantize(3, 2)
+        store_codes(2, 4)
+        store_scales(early_scales, 0, EARLY * P, [nc.sync] * 4)
+        y_quantize(4, 0)
+        y_quantize(4, 1)
+        scale(5, 2, G)
+        store_y(5, 0, CHUNKS)
+        tanh(6, 0)
+        matmuls(6, 2)
+        add_bias(6, 1)
+        tanh(6, 1)
+        y_transposes(4, (2,), "y_bank_1")
+        y_transposes(5, LOW, "y_bank_0")
+        add_bias(6, 2)
+        scale(6, 0, G)
+        matmuls(7, 0)
+        tanh(6, 2)
+        round_y(5, 2)
+        y_copy(4, (2,), V)
+        y_copy(5, LOW, V)
+        matmuls(7, 1)
+        scale(6, 1, G)
+        add_bias(7, 0)
+        round_y(6, 0)
+        tanh(7, 0)
+        matmuls(7, 2)
+        add_bias(7, 1)
+        y_quantize(4, 2)
+        store_codes(4, 5)
+        y_quantize(5, 0)
+        y_quantize(5, 1)
+        tanh(7, 1)
+        store_y(6, 0, 2)
+        round_y(6, 1)
+        y_transposes(5, (2,), "y_bank_1")
+        y_transposes(6, LOW, "y_bank_0")
+
+        halves = ((0, CHUNK // 2), (CHUNK // 2, CHUNK))
         for lo, hi in halves:
-            add_bias(t, 2, lo, hi)
-            tanh(t, 2, lo, hi)
-        scale(t, 0, nc.vector)
-        store_y(t, 0, 1)
-        scale(t, 1, nc.vector)
-        store_y(t, 1, 2)
-        round_y(t, 0, nc.scalar)
-        y_transposes(t, (0,), "x_bank_1")
-        round_y(t, 1, nc.scalar)
-        y_transposes(t, (1,), "acc")
+            add_bias(7, 2, lo, hi)
+            tanh(7, 2, lo, hi)
+        scale(6, 2, V)
+        store_y(6, 2, 3)
+        scale(7, 0, V)
+        scale(7, 1, V)
+        store_y(7, 0, 2)
+        round_y(6, 2)
+        y_transposes(6, (2,), "x_bank_0")
+        round_y(7, 0)
+        y_transposes(7, (0,), "x_bank_1")
         for lo, hi in halves:
-            scale_round(t, 2, lo, hi)
-        y_transposes(t, (2,), "acc")
-        scale(t, 2, nc.vector)
-        store_y(t, 2, 3)
-        y_copy(t - 1, LOW, nc.scalar)
-        y_copy(t - 2, (2,), nc.vector)
-        y_copy(t, (0,), nc.vector)
-        y_copy(t, (1,), nc.scalar)
-        y_quantize(t - 2, 2)
-        store_codes(t - 2, t - 1)
-        y_copy(t - 1, (2,), nc.scalar)
-        y_quantize(t - 1, 0)
-        y_quantize(t - 1, 1)
-        y_copy(t, (2,), nc.scalar)
-        y_quantize(t, 0)
-        y_quantize(t, 1)
-        store_codes(t - 1, t + 1, slice(0, 2))
-        y_quantize(t - 1, 2)
-        y_quantize(t, 2)
-        store_codes(t - 1, t + 1, slice(2, 3))
+            scale_round(7, 2, lo, hi)
+        round_y(7, 1)
+        y_transposes(7, (2,), "acc")
+        y_transposes(7, (1,), "acc")
+        scale(7, 2, V)
+        store_y(7, 2, 3)
+        y_copy(5, (2,), V)
+        y_copy(6, LOW, S)
+        y_copy(6, (2,), V)
+        y_copy(7, (0,), S)
+        y_copy(7, (2,), S)
+        y_copy(7, (1,), S)
+        for c, first in ((0, 6), (2, 5), (1, 6)):
+            for t in range(first, TILES):
+                y_quantize(t, c)
+            store_codes(5, TILES, slice(c, c + 1))
         store_scales(last_scales, EARLY * P, B, [nc.sync, nc.scalar] * 2)

from contextlib import ExitStack

import concourse.mybir as mybir
from concourse.masks import make_identity

B, R, U = 1024, 1536, 512
FLOPS = 2 * B * (R + U) * R

F32 = mybir.dt.float32
BF16 = mybir.dt.bfloat16
I32 = mybir.dt.int32
U32 = mybir.dt.uint32
U8 = mybir.dt.uint8
FP8X4 = mybir.dt.float8_e4m3fn_x4
FP4X4 = mybir.dt.float4_e2m1fn_x4
ALU = mybir.AluOpType
ACT = mybir.ActivationFunctionType

P = 128
K_PASS = 512
CHUNK = 512
PAIRS = K_PASS // 2
W_BYTES = 2 * CHUNK
TILES = B // P
CHUNKS = R // CHUNK
H_PASSES = R // K_PASS
LOW, HIGH = (0, 1), (2, 3)
ALL = LOW + HIGH
ACC_BANKS = 4
EARLY = TILES // 2


def tile_reservoir_state_step_g4_kernel(
    tc, h, u, wr_words, wr_scales, win_words, win_scales, bias, amp, out_0, out_1, out_2
):
    nc = tc.nc
    V, S, G = nc.vector, nc.scalar, nc.gpsimd
    with ExitStack() as ctx:
        keep = ctx.enter_context(tc.tile_pool(name="keep", bufs=1))
        work = ctx.enter_context(tc.tile_pool(name="work", bufs=4))
        psum = ctx.enter_context(tc.psum_pool(name="psum", bufs=1))
        ctx.enter_context(tc.manual_schedule())

        ident = keep.tile([P, P], F32, name="ident")
        make_identity(nc, ident[:])

        wr_sc = keep.tile([P, H_PASSES, R], U8, name="wr_sc", align_bytes=64)
        win_sc = keep.tile([P, R], U8, name="win_sc", align_bytes=64)
        V.memset(wr_sc[:].bitcast(I32), 0)
        V.memset(win_sc[:].bitcast(I32), 0)

        h_rows, x_pairs, w_codes = {}, {}, {}

        def load_column(name, vec):
            col = keep.tile([P, CHUNKS, 4], BF16, name=name)
            nc.sync.dma_start(out=col[:], in_=vec.rearrange("(c p j) -> p c j", c=CHUNKS, j=4))
            return col

        def load_x(t):
            rows = slice(t * P, (t + 1) * P)
            h_rows[t] = keep.tile([P, R], BF16, name="h_rows_%d" % t)
            nc.sync.dma_start(out=h_rows[t][:], in_=h[rows, :])
            u_rows = keep.tile([P, U], BF16, name="u_rows_%d" % t)
            nc.sync.dma_start(out=u_rows[:], in_=u[rows, :])
            for g in range(H_PASSES):
                x_pairs[t, g] = h_rows[t][:].bitcast(F32)[:, g * PAIRS : (g + 1) * PAIRS]
            x_pairs[t, H_PASSES] = u_rows[:].bitcast(F32)

        def load_wr(c):
            codes = keep.tile([P, H_PASSES, W_BYTES], U8, name="wr_%d" % c, align_bytes=64)
            src = wr_words[:, :, c * W_BYTES : (c + 1) * W_BYTES].rearrange("g p n -> p g n")
            nc.sync.dma_start(out=codes[:].bitcast(I32), in_=src.bitcast(I32))
            for g in range(H_PASSES):
                w_codes[g, c] = codes[:, g, :]

        def load_win(first, last):
            codes = keep.tile([P, (last - first) * W_BYTES], U8, name="win_%d" % first, align_bytes=64)
            src = win_words[0, :, first * W_BYTES : last * W_BYTES]
            nc.sync.dma_start(out=codes[:].bitcast(I32), in_=src.bitcast(I32))
            for c in range(first, last):
                w_codes[H_PASSES, c] = codes[:, (c - first) * W_BYTES : (c - first + 1) * W_BYTES]

        bias_col = load_column("bias_col", bias)
        load_x(0)
        for r in range(4):
            src = wr_scales[:, r::4, :].rearrange("g q n -> q g n")
            nc.sync.dma_start(out=wr_sc[r:P:32].bitcast(I32), in_=src.bitcast(I32))
        load_wr(0)
        load_win(0, 1)
        for r in range(4):
            nc.sync.dma_start(out=win_sc[r:P:32].bitcast(I32), in_=win_scales[0, r::4, :].bitcast(I32))
        load_x(1)
        amp_col = load_column("amp_col", amp)
        load_wr(1)
        load_win(1, CHUNKS)
        load_wr(2)
        for t in range(2, TILES):
            load_x(t)

        def bank_tile(name):
            return psum.tile([P, 512], F32, name=name, bufs=ACC_BANKS if name == "acc" else 1)

        def copy(engine, out, in_):
            if engine is S:
                S.copy(out=out, in_=in_)
            else:
                V.tensor_copy(out=out, in_=in_)

        def interleave(engine, dst, bank, groups):
            copy(
                engine,
                dst.bitcast(F32).rearrange("p (g m w) -> p g m w", g=groups, w=2),
                bank[:, : groups * 2 * P].rearrange("p (g w m) -> p g m w", g=groups, w=2),
            )

        def spread(col, rows):
            pairs = col[:].bitcast(F32)
            for name, chunks in (("y_bank_0", LOW), ("y_bank_1", (2,))):
                bank = bank_tile(name)
                for i, c in enumerate(chunks):
                    for w in range(2):
                        at = (2 * i + w) * P
                        repeated = pairs[:, c, w : w + 1].to_broadcast([P, P])
                        nc.tensor.transpose(bank[:, at : at + P], repeated, ident[:])
                interleave(S, rows[:, chunks[0] * CHUNK : (chunks[-1] + 1) * CHUNK], bank, len(chunks))

        x_sorted, x_bank, x_grouped, x_codes, x_scales = {}, {}, {}, {}, {}

        def x_sort(t, count):
            ordered = work.tile([P, count, 2, P], F32, name="x_sorted", bufs=3)
            src = h_rows[t][:].bitcast(F32)[:, : count * PAIRS].rearrange("p (g j w) -> p g w j", g=count, w=2)
            V.tensor_copy(out=ordered[:], in_=src)
            for g in range(count):
                x_sorted[t, g] = ordered[:, g]

        def x_transposes(t, passes, name):
            bank = bank_tile(name)
            for i, g in enumerate(passes):
                for w in range(2):
                    at = (2 * i + w) * P
                    pairs = x_sorted[t, g][:, w, :] if (t, g) in x_sorted else x_pairs[t, g][:, w::2]
                    nc.tensor.transpose(bank[:, at : at + P], pairs, ident[:])
            x_bank[t, passes] = bank

        def x_run(t):
            x_transposes(t, LOW, "x_bank_0")
            x_transposes(t, HIGH, "x_bank_1")

        def x_copy(t, passes, engine, together=ALL):
            if (t, together) not in x_grouped:
                x_grouped[t, together] = work.tile([P, len(together) * K_PASS], BF16, name="x_grouped", align_bytes=64)
            at = (passes[0] - together[0]) * K_PASS
            dst = x_grouped[t, together][:, at : at + len(passes) * K_PASS]
            interleave(engine, dst, x_bank[t, passes], len(passes))

        def x_quantize(t, passes=ALL):
            codes = work.tile([P, len(passes) * P], U32, name="x_codes", align_bytes=64, bufs=6)
            scales = work.tile([P, len(passes) * P], U8, name="x_scales", align_bytes=64, bufs=6)
            V.quantize_mx(out=codes[:].bitcast(FP8X4), scales=scales[:], in_=x_grouped[t, passes][:])
            for i, g in enumerate(passes):
                x_codes[t, g] = codes[:, i * P : (i + 1) * P]
                x_scales[t, g] = scales[:, i * P : (i + 1) * P]

        acc, pre, y_rows, y_bf, y_bank, y_grouped = {}, {}, {}, {}, {}, {}

        def matmuls(t, c):
            cols = slice(c * CHUNK, (c + 1) * CHUNK)
            acc[t, c] = bank_tile("acc")
            for g in ALL:
                nc.tensor.matmul_mx(
                    out=acc[t, c][:],
                    lhsT=x_codes[t, g].bitcast(FP8X4),
                    lhsT_scale=x_scales[t, g],
                    rhs=w_codes[g, c].bitcast(FP4X4),
                    rhs_scale=wr_sc[:, g, cols] if g < H_PASSES else win_sc[:, cols],
                    start=(g == ALL[0]),
                    stop=(g == ALL[-1]),
                )

        def add_bias(t, c, lo=0, hi=CHUNK):
            if lo == 0:
                pre[t, c] = work.tile([P, CHUNK], F32, name="pre")
            V.tensor_tensor(
                out=pre[t, c][:, lo:hi],
                in0=acc[t, c][:, lo:hi],
                in1=bias_rows[:, c * CHUNK + lo : c * CHUNK + hi],
                op=ALU.add,
            )

        def tanh(t, c, lo=0, hi=CHUNK):
            S.activation(out=pre[t, c][:, lo:hi], in_=pre[t, c][:, lo:hi], func=ACT.Tanh)

        def scale(t, c, engine):
            if c == 0:
                y_rows[t] = work.tile([P, R], F32, name="y_rows")
            cols = slice(c * CHUNK, (c + 1) * CHUNK)
            engine.tensor_tensor(out=y_rows[t][:, cols], in0=pre[t, c][:], in1=amp_rows[:, cols], op=ALU.mult)

        def store_y(t, first, last):
            cols = slice(first * CHUNK, last * CHUNK)
            nc.sync.dma_start(out=out_0[t * P : (t + 1) * P, cols], in_=y_rows[t][:, cols])

        def by_pair(values):
            return values.rearrange("p (j w e) -> p w j e", w=2, e=2)

        def rounded_tile(t, c):
            y_bf[t, c] = work.tile([P, CHUNK], BF16, name="y_bf", bufs=6)

        def rounded_view(t, c):
            return y_bf[t, c][:].rearrange("p (w j e) -> p w j e", w=2, e=2)

        def round_y(t, c):
            rounded_tile(t, c)
            S.copy(out=rounded_view(t, c), in_=by_pair(y_rows[t][:, c * CHUNK : (c + 1) * CHUNK]))

        def scale_round(t, c, lo, hi):
            if lo == 0:
                rounded_tile(t, c)
            js = slice(lo // 4, hi // 4)
            V.tensor_tensor(
                out=rounded_view(t, c)[:, :, js],
                in0=by_pair(pre[t, c][:])[:, :, js],
                in1=by_pair(amp_rows[:, c * CHUNK : (c + 1) * CHUNK])[:, :, js],
                op=ALU.mult,
            )

        def y_transposes(t, chunks, name):
            bank = bank_tile(name)
            for i, c in enumerate(chunks):
                pairs = y_bf[t, c][:].bitcast(F32)
                for w in range(2):
                    at = (2 * i + w) * P
                    nc.tensor.transpose(bank[:, at : at + P], pairs[:, w * P : (w + 1) * P], ident[:])
            y_bank[t, chunks] = bank

        def y_copy(t, chunks, engine):
            grouped = work.tile([P, len(chunks) * CHUNK], BF16, name="y_grouped", align_bytes=64, bufs=8)
            interleave(engine, grouped[:], y_bank[t, chunks], len(chunks))
            for i, c in enumerate(chunks):
                y_grouped[t, c] = grouped[:, i * CHUNK : (i + 1) * CHUNK]

        y_codes = keep.tile([P, CHUNKS, B], U32, name="y_codes", align_bytes=64)
        early_scales = keep.tile([P, CHUNKS, EARLY * P], U8, name="early_scales", align_bytes=64)
        last_scales = keep.tile([P, CHUNKS, B - EARLY * P], U8, name="last_scales", align_bytes=64)

        def y_quantize(t, c):
            scales, at = (early_scales, t * P) if t < EARLY else (last_scales, (t - EARLY) * P)
            V.quantize_mx(
                out=y_codes[:, c, t * P : (t + 1) * P].bitcast(FP8X4),
                scales=scales[:, c, at : at + P],
                in_=y_grouped[t, c],
            )

        def store_codes(first, last, chunks=slice(0, CHUNKS)):
            dst = out_1.rearrange("g p m j -> p g (m j)")[:, chunks, first * 4 * P : last * 4 * P]
            nc.sync.dma_start(out=dst.bitcast(I32), in_=y_codes[:, chunks, first * P : last * P].bitcast(I32))

        def store_scales(scales, lo, hi, queues):
            for a in range(4):
                dst = out_2[:, 4 * a : 4 * a + 4, lo:hi].rearrange("g r m -> r g m")
                queues[a].dma_start(out=dst.bitcast(I32), in_=scales[32 * a : 32 * a + 4].bitcast(I32))

        bias_rows = keep.tile([P, R], BF16, name="bias_rows")
        amp_rows = keep.tile([P, R], BF16, name="amp_rows")
        spread(bias_col, bias_rows)
        for g, name in zip(ALL, ("x_bank_0", "x_bank_1", "acc", "acc")):
            x_transposes(0, (g,), name)
        for first, second in (LOW, HIGH):
            x_copy(0, (first,), V, (first,))
            x_copy(0, (second,), S, (second,))
            x_quantize(0, (first,))
            x_quantize(0, (second,))

        for t in range(TILES - 2):
            matmuls(t, 0)
            if t >= 1:
                scale(t - 1, 1, G)
                add_bias(t - 1, 2)
                if t == 1:
                    x_sort(3, H_PASSES)
                round_y(t - 1, 0)
                tanh(t - 1, 2)
                round_y(t - 1, 1)
            add_bias(t, 0)
            if t == 0:
                x_run(1)
                spread(amp_col, amp_rows)
            matmuls(t, 1)
            tanh(t, 0)
            if t == 0:
                x_copy(1, LOW, V)
                x_copy(1, HIGH, V)
                x_quantize(1)
            if t >= 3:
                y_quantize(t - 3, 2)
                if t % 2 == 0:
                    store_codes(t - 4, t - 2)
            if t >= 2:
                y_quantize(t - 2, 0)
                y_quantize(t - 2, 1)
            if t >= 1:
                x_quantize(t + 1)
                if t + 3 < TILES:
                    x_sort(t + 3, H_PASSES if t == 1 else 1)
                scale(t - 1, 2, G)
                store_y(t - 1, 0, CHUNKS)
            add_bias(t, 1)
            if t == 0:
                matmuls(t, 2)
            x_run(t + 2)
            if t >= 2:
                y_transposes(t - 2, (2,), "y_bank_1")
            if t >= 1:
                y_transposes(t - 1, LOW, "y_bank_0")
                matmuls(t, 2)
            if t == 0:
                tanh(t, 1)
            x_copy(t + 2, LOW, S)
            if t >= 1:
                tanh(t, 1)
            x_copy(t + 2, HIGH, S)
            if t >= 2:
                y_copy(t - 2, (2,), V)
            if t >= 1:
                y_copy(t - 1, LOW, V)
            scale(t, 0, V)
            if t >= 1:
                round_y(t - 1, 2)

        matmuls(6, 0)
        add_bias(5, 2)
        tanh(5, 2)
        scale(5, 1, V)
        round_y(5, 0)
        matmuls(6, 1)
        add_bias(6, 0)
        round_y(5, 1)
        x_quantize(7)
        y_quantize(3, 2)
        store_codes(2, 4)
        store_scales(early_scales, 0, EARLY * P, [nc.sync] * 4)
        y_quantize(4, 0)
        y_quantize(4, 1)
        scale(5, 2, G)
        store_y(5, 0, CHUNKS)
        tanh(6, 0)
        matmuls(6, 2)
        add_bias(6, 1)
        tanh(6, 1)
        y_transposes(4, (2,), "y_bank_1")
        y_transposes(5, LOW, "y_bank_0")
        add_bias(6, 2)
        scale(6, 0, G)
        matmuls(7, 0)
        tanh(6, 2)
        round_y(5, 2)
        y_copy(4, (2,), V)
        y_copy(5, LOW, V)
        matmuls(7, 1)
        scale(6, 1, G)
        add_bias(7, 0)
        round_y(6, 0)
        tanh(7, 0)
        matmuls(7, 2)
        add_bias(7, 1)
        y_quantize(4, 2)
        store_codes(4, 5)
        y_quantize(5, 0)
        y_quantize(5, 1)
        tanh(7, 1)
        store_y(6, 0, 2)
        round_y(6, 1)
        y_transposes(5, (2,), "y_bank_1")
        y_transposes(6, LOW, "y_bank_0")

        halves = ((0, CHUNK // 2), (CHUNK // 2, CHUNK))
        for lo, hi in halves:
            add_bias(7, 2, lo, hi)
            tanh(7, 2, lo, hi)
        scale(6, 2, V)
        store_y(6, 2, 3)
        scale(7, 0, V)
        scale(7, 1, V)
        store_y(7, 0, 2)
        round_y(6, 2)
        y_transposes(6, (2,), "x_bank_0")
        round_y(7, 0)
        y_transposes(7, (0,), "x_bank_1")
        for lo, hi in halves:
            scale_round(7, 2, lo, hi)
        round_y(7, 1)
        y_transposes(7, (2,), "acc")
        y_transposes(7, (1,), "acc")
        scale(7, 2, V)
        store_y(7, 2, 3)
        y_copy(5, (2,), V)
        y_copy(6, LOW, S)
        y_copy(6, (2,), V)
        y_copy(7, (0,), S)
        y_copy(7, (2,), S)
        y_copy(7, (1,), S)
        for c, first in ((0, 6), (2, 5), (1, 6)):
            for t in range(first, TILES):
                y_quantize(t, c)
            store_codes(5, TILES, slice(c, c + 1))
        store_scales(last_scales, EARLY * P, B, [nc.sync, nc.scalar] * 2)
